import numpy as np
import ml_dtypes


def mxq(x, axis, fmt="e4m3"):
    dtype, down = {"e4m3": (ml_dtypes.float8_e4m3fn, 7), "e5m2": (ml_dtypes.float8_e5m2, 14)}[fmt]
    v = np.moveaxis(np.asarray(x, np.float32).astype(ml_dtypes.bfloat16).astype(np.float64), axis, -1)
    blocks = v.reshape(v.shape[:-1] + (-1, 32))
    amax = np.abs(blocks).max(-1, keepdims=True)
    byte = np.maximum(np.where(amax > 0, np.frexp(amax)[1] - 1 + 127, 0) - down, 1)
    scale = np.exp2(byte - 127.0)
    codes = (blocks / scale).astype(np.float32).astype(dtype).astype(np.float64)
    return np.moveaxis((codes * scale).reshape(v.shape), -1, axis)


WIDE = False


def mx_kscale(k):
    if not WIDE:
        return np.ones(k)
    levels = np.array([10, -10, 5, -5, 0])
    if k % 512:
        return np.exp2(np.random.permutation(np.resize(levels, k // 32))).repeat(32)
    a = np.empty((k // 512, 16))
    for p in range(k // 512):
        a[p, :8] = np.random.permutation(np.resize(levels, 8))
        for g in range(8):
            far = levels[np.abs(levels - a[p, g]) >= 10]
            a[p, g + 8] = far[np.random.randint(len(far))]
    return np.exp2(a.ravel()).repeat(32)


def f64(x):
    return np.asarray(x).astype(np.float64)


def striped(idx):
    return np.tile(idx.reshape(-1, 16).T, (8, 1)).astype(np.uint16)


def unstriped(offs):
    return offs[:16].T.reshape(-1).astype(np.int64)


def pack_weight(w):
    k, n = w.shape
    w = f64(np.asarray(w, np.float32).astype(ml_dtypes.bfloat16)).reshape(k // 32, 32, n)
    amax = np.abs(w).max(1)
    byte = np.clip(np.where(amax > 0, np.frexp(amax)[1] - 1 + 127 - 7, 1), 1, 254)
    scaled = (w * np.exp2(127.0 - byte)[:, None, :]).reshape(k, n).astype(np.float32)
    words = np.ascontiguousarray(scaled.reshape(k // 512, 128, 4, n).transpose(0, 1, 3, 2)).astype(ml_dtypes.float8_e4m3fn).view(np.uint8)
    return words, np.ascontiguousarray(byte.astype(np.uint8).reshape(k // 512, 16, n))


def unpack_weight(words, scales):
    g, p, n, _ = words.shape
    vals = np.ascontiguousarray(words).view(ml_dtypes.float8_e4m3fn).astype(np.float64) * np.repeat(np.exp2(scales.astype(np.float64) - 127.0), 8, axis=1)[..., None]
    return vals.transpose(0, 1, 3, 2).reshape(g * 512, n)


def relu(v):
    return np.maximum(v, 0.0)


K, T, S, V, H, N = 512, 2048, 1024, 512, 512, 128


def setup_inputs():
    n = np.random.standard_normal
    s = mx_kscale(K)[:, None]
    u = mx_kscale(H)
    packed_xT = pack_weight(n((K, T)) * s)
    packed_w2 = pack_weight(n((H, N)) / np.sqrt(2 * H) / u[:, None])
    packed_w3 = pack_weight(n((H, N)) / np.sqrt(2 * H) / u[:, None])
    return {
        "x_words": packed_xT[0],
        "x_scales": packed_xT[1],
        "w1": (n((K, H)) / np.sqrt(K) / s * u).astype(np.float32),
        "w2_words": packed_w2[0],
        "w2_scales": packed_w2[1],
        "w3_words": packed_w3[0],
        "w3_scales": packed_w3[1],
        "offs": striped(np.random.permutation(T)[:S]),
        "cen": striped(np.random.permutation(S)[:V]),
        "pos1": striped(np.random.permutation(S)[:V]),
        "pos2": striped(np.random.permutation(S)[:V]),
        "pos3": striped(np.random.permutation(S)[:V]),
        "pos4": striped(np.random.permutation(S)[:V]),
    }


def reference(x_words, x_scales, w1, w2_words, w2_scales, w3_words, w3_scales, offs, cen, pos1, pos2, pos3, pos4):
    xq = unpack_weight(x_words, x_scales)[:, unstriped(offs)]
    h = relu(mxq(f64(w1), 0, "e4m3").T @ xq)
    hc = h[:, unstriped(cen)]
    z = np.maximum(np.maximum(np.maximum(h[:, unstriped(pos1)], h[:, unstriped(pos2)]), h[:, unstriped(pos3)]), h[:, unstriped(pos4)])
    return relu(unpack_weight(w2_words, w2_scales).T @ mxq(hc, 0, "e4m3") + unpack_weight(w3_words, w3_scales).T @ mxq(z, 0, "e4m3"))

@@ -1,0 +1,178 @@
+from contextlib import ExitStack
+
+import concourse.mybir as mybir
+
+K, T, S, V, H, N = 512, 2048, 1024, 512, 512, 128
+FLOPS = 2 * K * H * S + 2 * 2 * H * N * V
+
+F32 = mybir.dt.float32
+BF16 = mybir.dt.bfloat16
+I32 = mybir.dt.int32
+U32 = mybir.dt.uint32
+U16 = mybir.dt.uint16
+U8 = mybir.dt.uint8
+FP8X4 = mybir.dt.float8_e4m3fn_x4
+RELU = mybir.ActivationFunctionType.Relu
+MAX = mybir.AluOpType.max
+
+P = 128
+PACK = 4
+BANK = 512
+LIST_ROWS = 16
+TAIL = 128
+HALF = V // 2
+
+
+def load_scale_rows(queue, plane, scales):
+    for q in range(4):
+        queue.dma_start(out=plane[32 * q : 32 * q + 4, :].bitcast(I32), in_=scales[0, 4 * q : 4 * q + 4, :].bitcast(I32))
+
+
+def words_of(dram_words):
+    return dram_words[0].rearrange("p n t -> p (n t)").bitcast(I32)
+
+
+def entries(offsets, first, last):
+    return offsets[:, first // LIST_ROWS : last // LIST_ROWS]
+
+
+def tile_picked_sagecat_maxrelu_p_kernel(
+    tc, x_words, x_scales, w1, w2_words, w2_scales, w3_words, w3_scales, offs, cen, pos1, pos2, pos3, pos4, out
+):
+    nc = tc.nc
+    with ExitStack() as ctx:
+        lists = ctx.enter_context(tc.tile_pool(name="lists", bufs=1))
+        keep = ctx.enter_context(tc.tile_pool(name="keep", bufs=1))
+        ring = ctx.enter_context(tc.tile_pool(name="ring", bufs=2))
+        psum_h = ctx.enter_context(tc.psum_pool(name="psum_h", bufs=6))
+        psum_out = ctx.enter_context(tc.psum_pool(name="psum_out", bufs=2))
+
+        xs_all = keep.tile([P, T], U8, name="xs_all", align_bytes=64)
+        nc.vector.memset(xs_all[:, : T // 2].bitcast(I32), 0)
+        nc.gpsimd.memset(xs_all[:, T // 2 :].bitcast(I32), 0)
+        offs_sb = lists.tile([P, S // LIST_ROWS], U16, name="offs_sb")
+        pos_sb = [lists.tile([P, V // LIST_ROWS], U16, name="pos_sb%d" % d) for d in range(4)]
+        cen_sb = lists.tile([P, V // LIST_ROWS], U16, name="cen_sb")
+        w1_rows = w1.rearrange("(p j) c -> p j c", j=PACK)
+        w1_parts = ((0, 320), (320, H))
+        w1_raw = [keep.tile([P, PACK, c1 - c0], F32, name="w1_raw%d" % c0) for c0, c1 in w1_parts]
+        nc.sync.dma_start(out=w1_raw[0][:], in_=w1_rows[:, :, :320])
+        nc.sync.dma_start(offs_sb[:], offs)
+        load_scale_rows(nc.sync, xs_all, x_scales)
+        xw_all = keep.tile([P, T], I32, name="xw_all", align_bytes=64)
+        nc.sync.dma_start(out=xw_all[:], in_=words_of(x_words))
+        nc.sync.dma_start(out=w1_raw[1][:], in_=w1_rows[:, :, 320:])
+        nc.sync.dma_start(pos_sb[0][:], pos1)
+        nc.sync.dma_start(pos_sb[1][:], pos2)
+        nc.sync.dma_start(pos_sb[2][:], pos3)
+        nc.sync.dma_start(pos_sb[3][:], pos4)
+        nc.sync.dma_start(cen_sb[:], cen)
+
+        w2_codes = keep.tile([P, N], I32, name="w2_codes", align_bytes=64)
+        w3_codes = keep.tile([P, N], I32, name="w3_codes", align_bytes=64)
+        w2_plane = keep.tile([P, N], U8, name="w2_plane", align_bytes=64)
+        w3_plane = keep.tile([P, N], U8, name="w3_plane", align_bytes=64)
+        for codes, plane, words, scales in ((w3_codes, w3_plane, w3_words, w3_scales), (w2_codes, w2_plane, w2_words, w2_scales)):
+            nc.sync.dma_start(out=codes[:], in_=words_of(words))
+            nc.gpsimd.memset(plane[:].bitcast(I32), 0)
+            load_scale_rows(nc.sync, plane, scales)
+
+        xs_pick = keep.tile([P, S], U8, name="xs_pick", align_bytes=64)
+        nc.vector.tensor_copy(xs_pick[:], xs_all[:].indirect(offs_sb[:]))
+        xw_window = xw_all[:].bitcast(U32)
+        xw_first = keep.tile([P, BANK], U32, name="xw_first", align_bytes=64)
+        nc.vector.tensor_copy(xw_first[:], xw_window.indirect(entries(offs_sb, 0, BANK)))
+
+        w1_grouped = keep.tile([P, PACK, P, PACK], BF16, name="w1_grouped", tag="w1_then_x", align_bytes=64)
+        for raw, (c0, c1) in zip(w1_raw, w1_parts):
+            nc.scalar.copy(
+                w1_grouped[:, :, c0 // PACK : c1 // PACK, :].rearrange("p t m j -> p m t j"),
+                raw[:].rearrange("p j (m t) -> p m t j", t=PACK),
+            )
+        w1_codes = keep.tile([P, H], U32, name="w1_codes", align_bytes=64)
+        w1_plane = keep.tile([P, H], U8, name="w1_plane", align_bytes=64)
+        nc.vector.quantize_mx(out=w1_codes[:].bitcast(FP8X4), scales=w1_plane[:], in_=w1_grouped[:].rearrange("p t m j -> p (t m j)"))
+        xw_second = keep.tile([P, BANK], U32, name="xw_second", tag="w1_then_x", align_bytes=64)
+        for first in (0, BANK // 2):
+            nc.vector.tensor_copy(
+                xw_second[:, first : first + BANK // 2], xw_window.indirect(entries(offs_sb, BANK + first, BANK + first + BANK // 2))
+            )
+        h = []
+        for t in range(PACK):
+            h_t = keep.tile([P, S], F32, name="h%d" % t, align_bytes=64)
+            width = BANK // 2 if t == 0 else BANK
+            pieces = [(xw_first[:], 0, BANK)] + [(xw_second[:, c : c + width], BANK + c, width) for c in range(0, BANK, width)]
+            for words, first, count in pieces:
+                acc = psum_h.tile([P, count], F32, name="acc_h")
+                nc.tensor.matmul_mx(
+                    out=acc[:], lhsT=w1_codes[:, t * P : (t + 1) * P].bitcast(FP8X4), lhsT_scale=w1_plane[:, t * P : (t + 1) * P],
+                    rhs=words.bitcast(FP8X4), rhs_scale=xs_pick[:, first : first + count], start=True, stop=True,
+                )
+                nc.scalar.activation(h_t[:, first : first + count], acc[:], RELU)
+            h.append(h_t)
+
+        z_planes = keep.tile([P, PACK, V], BF16, name="z_planes", align_bytes=64)
+        c_planes = keep.tile([P, 2, V], BF16, name="c_planes", align_bytes=64)
+        z_in = [keep.tile([P, HALF, PACK], BF16, name="z_in%d" % half, tag="mx_in%d" % half, align_bytes=64) for half in range(2)]
+        c_in = [keep.tile([P, HALF, PACK], BF16, name="c_in0", align_bytes=64)]
+
+        def weave(dst, planes, t0, half):
+            nc.scalar.copy(dst[:, :, t0 : t0 + 2], planes[:, t0 : t0 + 2, half * HALF : (half + 1) * HALF].rearrange("p t v -> p v t"))
+
+        def quantize(values, name):
+            codes = keep.tile([P, HALF], U32, name=name + "_codes", align_bytes=64)
+            plane = keep.tile([P, HALF], U8, name=name + "_plane", align_bytes=64)
+            nc.vector.quantize_mx(out=codes[:].bitcast(FP8X4), scales=plane[:], in_=values[:].rearrange("p v t -> p (v t)"))
+            return codes, plane
+
+        pending = None
+        for t in range(PACK):
+            near = ring.tile([P, 4, V], BF16, name="near")
+            for d in range(4):
+                nc.vector.tensor_copy(near[:, d, :], h[t][:].indirect(pos_sb[d][:]))
+                if d == 0 and pending is not None:
+                    pending()
+            if t < 2:
+                nc.vector.tensor_copy(c_planes[:, t, :], h[t][:].indirect(cen_sb[:]))
+            if t < 3:
+                pair = ring.tile([P, 2, V], BF16, name="pair")
+            else:
+                pair = keep.tile([P, 2, V], BF16, name="pair_last", tag="pair_last", align_bytes=64)
+            nc.vector.tensor_tensor(pair[:], near[:, 0:2, :], near[:, 2:4, :], MAX)
+
+            def finish(t=t, pair=pair):
+                nc.vector.tensor_tensor(z_planes[:, t, :], pair[:, 0, :], pair[:, 1, :], MAX)
+                if t == 1:
+                    weave(z_in[0], z_planes, 0, 0)
+                    weave(z_in[1], z_planes, 0, 1)
+                    weave(c_in[0], c_planes, 0, 0)
+
+            pending = finish
+        pending()
+        c_late = keep.tile([P, 2, HALF], BF16, name="c_late", tag="pair_last", align_bytes=64)
+        for t in (2, 3):
+            nc.vector.tensor_copy(c_late[:, t - 2, :], h[t][:].indirect(entries(cen_sb, 0, HALF)))
+        acc = []
+        for half in range(2):
+            weave(z_in[half], z_planes, 2, half)
+            codes, plane = quantize(z_in[half], "z%d" % half)
+            bank = psum_out.tile([P, HALF], F32, name="acc_out")
+            nc.tensor.matmul_mx(
+                out=bank[:], lhsT=w3_codes[:].bitcast(FP8X4), lhsT_scale=w3_plane[:],
+                rhs=codes[:].bitcast(FP8X4), rhs_scale=plane[:], start=True, stop=False,
+            )
+            acc.append(bank)
+        nc.scalar.copy(c_in[0][:, :, 2:4], c_late[:].rearrange("p t v -> p v t"))
+        c_in.append(keep.tile([P, HALF, PACK], BF16, name="c_in1", tag="mx_in1", align_bytes=64))
+        weave(c_in[1], c_planes, 0, 1)
+        for t in (2, 3):
+            nc.vector.tensor_copy(c_in[1][:, :, t], h[t][:].indirect(entries(cen_sb, HALF, V)))
+        for half in range(2):
+            codes, plane = quantize(c_in[half], "c%d" % half)
+            nc.tensor.matmul_mx(
+                out=acc[half][:], lhsT=w2_codes[:].bitcast(FP8X4), lhsT_scale=w2_plane[:],
+                rhs=codes[:].bitcast(FP8X4), rhs_scale=plane[:], start=False, stop=True,
+            )
+            result = keep.tile([P, HALF], F32, name="result%d" % half)
+            nc.scalar.activation(result[:], acc[half][:], RELU)
+            nc.sync.dma_start(out=out[:, half * HALF : (half + 1) * HALF], in_=result[:])

@@ -19,7 +19,7 @@ P = 128
 PACK = 4
 BANK = 512
 LIST_ROWS = 16
-TAIL = 128
+LAST = 256
 HALF = V // 2
 
 
@@ -44,8 +44,8 @@ def tile_picked_sagecat_maxrelu_p_kernel(
         lists = ctx.enter_context(tc.tile_pool(name="lists", bufs=1))
         keep = ctx.enter_context(tc.tile_pool(name="keep", bufs=1))
         ring = ctx.enter_context(tc.tile_pool(name="ring", bufs=2))
-        psum_h = ctx.enter_context(tc.psum_pool(name="psum_h", bufs=6))
-        psum_out = ctx.enter_context(tc.psum_pool(name="psum_out", bufs=2))
+        psum_h = ctx.enter_context(tc.psum_pool(name="psum_h", bufs=5))
+        psum_out = ctx.enter_context(tc.psum_pool(name="psum_out", bufs=3))
 
         xs_all = keep.tile([P, T], U8, name="xs_all", align_bytes=64)
         nc.vector.memset(xs_all[:, : T // 2].bitcast(I32), 0)
@@ -54,14 +54,14 @@ def tile_picked_sagecat_maxrelu_p_kernel(
         pos_sb = [lists.tile([P, V // LIST_ROWS], U16, name="pos_sb%d" % d) for d in range(4)]
         cen_sb = lists.tile([P, V // LIST_ROWS], U16, name="cen_sb")
         w1_rows = w1.rearrange("(p j) c -> p j c", j=PACK)
-        w1_parts = ((0, 320), (320, H))
+        w1_parts = ((0, 256), (256, H))
         w1_raw = [keep.tile([P, PACK, c1 - c0], F32, name="w1_raw%d" % c0) for c0, c1 in w1_parts]
-        nc.sync.dma_start(out=w1_raw[0][:], in_=w1_rows[:, :, :320])
+        nc.sync.dma_start(out=w1_raw[0][:], in_=w1_rows[:, :, :256])
         nc.sync.dma_start(offs_sb[:], offs)
         load_scale_rows(nc.sync, xs_all, x_scales)
         xw_all = keep.tile([P, T], I32, name="xw_all", align_bytes=64)
         nc.sync.dma_start(out=xw_all[:], in_=words_of(x_words))
-        nc.sync.dma_start(out=w1_raw[1][:], in_=w1_rows[:, :, 320:])
+        nc.sync.dma_start(out=w1_raw[1][:], in_=w1_rows[:, :, 256:])
         nc.sync.dma_start(pos_sb[0][:], pos1)
         nc.sync.dma_start(pos_sb[1][:], pos2)
         nc.sync.dma_start(pos_sb[2][:], pos3)
@@ -80,99 +80,106 @@ def tile_picked_sagecat_maxrelu_p_kernel(
         xs_pick = keep.tile([P, S], U8, name="xs_pick", align_bytes=64)
         nc.vector.tensor_copy(xs_pick[:], xs_all[:].indirect(offs_sb[:]))
         xw_window = xw_all[:].bitcast(U32)
-        xw_first = keep.tile([P, BANK], U32, name="xw_first", align_bytes=64)
-        nc.vector.tensor_copy(xw_first[:], xw_window.indirect(entries(offs_sb, 0, BANK)))
+        xw_early = keep.tile([P, S - LAST], U32, name="xw_early", align_bytes=64)
+        for first, last in ((0, BANK), (BANK, S - LAST)):
+            nc.vector.tensor_copy(xw_early[:, first:last], xw_window.indirect(entries(offs_sb, first, last)))
 
-        w1_grouped = keep.tile([P, PACK, P, PACK], BF16, name="w1_grouped", tag="w1_then_x", align_bytes=64)
+        w1_lead = keep.tile([P, 1, P, PACK], BF16, name="w1_lead", tag="w1_then_x", align_bytes=64)
+        w1_rest = keep.tile([P, PACK - 1, P, PACK], BF16, name="w1_rest", align_bytes=64)
         for raw, (c0, c1) in zip(w1_raw, w1_parts):
-            nc.scalar.copy(
-                w1_grouped[:, :, c0 // PACK : c1 // PACK, :].rearrange("p t m j -> p m t j"),
-                raw[:].rearrange("p j (m t) -> p m t j", t=PACK),
-            )
+            by_plane = raw[:].rearrange("p j (m t) -> p m t j", t=PACK)
+            for grouped, t0, t1 in ((w1_lead, 0, 1), (w1_rest, 1, PACK)):
+                nc.scalar.copy(grouped[:, :, c0 // PACK : c1 // PACK, :].rearrange("p t m j -> p m t j"), by_plane[:, :, t0:t1, :])
         w1_codes = keep.tile([P, H], U32, name="w1_codes", align_bytes=64)
         w1_plane = keep.tile([P, H], U8, name="w1_plane", align_bytes=64)
-        nc.vector.quantize_mx(out=w1_codes[:].bitcast(FP8X4), scales=w1_plane[:], in_=w1_grouped[:].rearrange("p t m j -> p (t m j)"))
-        xw_second = keep.tile([P, BANK], U32, name="xw_second", tag="w1_then_x", align_bytes=64)
-        for first in (0, BANK // 2):
-            nc.vector.tensor_copy(
-                xw_second[:, first : first + BANK // 2], xw_window.indirect(entries(offs_sb, BANK + first, BANK + first + BANK // 2))
-            )
+
+        def quantize_w1(t0, t1, grouped):
+            cols = slice(t0 * P, t1 * P)
+            nc.vector.quantize_mx(out=w1_codes[:, cols].bitcast(FP8X4), scales=w1_plane[:, cols], in_=grouped.rearrange("p t m j -> p (t m j)"))
+
+        quantize_w1(0, 1, w1_lead[:])
+        xw_late = keep.tile([P, LAST], U32, name="xw_late", tag="w1_then_x", align_bytes=64)
+        nc.vector.tensor_copy(xw_late[:], xw_window.indirect(entries(offs_sb, S - LAST, S)))
+        quantize_w1(1, 2, w1_rest[:, 0:1])
+        quantize_w1(2, 4, w1_rest[:, 1:3])
+        pieces = ((xw_early[:, :BANK], 0, BANK), (xw_early[:, BANK:], BANK, LAST), (xw_late[:], S - LAST, LAST))
         h = []
         for t in range(PACK):
             h_t = keep.tile([P, S], F32, name="h%d" % t, align_bytes=64)
-            width = BANK // 2 if t == 0 else BANK
-            pieces = [(xw_first[:], 0, BANK)] + [(xw_second[:, c : c + width], BANK + c, width) for c in range(0, BANK, width)]
-            for words, first, count in pieces:
-                acc = psum_h.tile([P, count], F32, name="acc_h")
+            banks = [psum_h.tile([P, BANK], F32, name="acc_h") for bank in range(3 if t == 0 else 2)]
+            for number, (words, first, count) in enumerate(pieces):
+                acc = banks[number][:, :count] if t == 0 or number == 0 else banks[1][:, first - BANK : first - BANK + count]
                 nc.tensor.matmul_mx(
-                    out=acc[:], lhsT=w1_codes[:, t * P : (t + 1) * P].bitcast(FP8X4), lhsT_scale=w1_plane[:, t * P : (t + 1) * P],
+                    out=acc, lhsT=w1_codes[:, t * P : (t + 1) * P].bitcast(FP8X4), lhsT_scale=w1_plane[:, t * P : (t + 1) * P],
                     rhs=words.bitcast(FP8X4), rhs_scale=xs_pick[:, first : first + count], start=True, stop=True,
                 )
-                nc.scalar.activation(h_t[:, first : first + count], acc[:], RELU)
+                if t == 0 and number == 2:
+                    nc.vector.tensor_scalar_max(h_t[:, first : first + count], acc, 0.0)
+                elif t == 0 or number == 0:
+                    nc.scalar.activation(h_t[:, first : first + count], acc, RELU)
+                elif number == 2:
+                    nc.scalar.activation(h_t[:, BANK:], banks[1][:], RELU)
             h.append(h_t)
 
         z_planes = keep.tile([P, PACK, V], BF16, name="z_planes", align_bytes=64)
-        c_planes = keep.tile([P, 2, V], BF16, name="c_planes", align_bytes=64)
-        z_in = [keep.tile([P, HALF, PACK], BF16, name="z_in%d" % half, tag="mx_in%d" % half, align_bytes=64) for half in range(2)]
-        c_in = [keep.tile([P, HALF, PACK], BF16, name="c_in0", align_bytes=64)]
+        c_planes = keep.tile([P, PACK, V], BF16, name="c_planes", align_bytes=64)
+        z_in = keep.tile([P, V, PACK], BF16, name="z_in", align_bytes=64)
+        c_in = keep.tile([P, V, PACK], BF16, name="c_in", align_bytes=64)
 
-        def weave(dst, planes, t0, half):
-            nc.scalar.copy(dst[:, :, t0 : t0 + 2], planes[:, t0 : t0 + 2, half * HALF : (half + 1) * HALF].rearrange("p t v -> p v t"))
+        def weave(dst, planes, t0, v0, v1):
+            nc.scalar.copy(dst[:, v0:v1, t0 : t0 + 2], planes[:, t0 : t0 + 2, v0:v1].rearrange("p t v -> p v t"))
 
-        def quantize(values, name):
-            codes = keep.tile([P, HALF], U32, name=name + "_codes", align_bytes=64)
-            plane = keep.tile([P, HALF], U8, name=name + "_plane", align_bytes=64)
-            nc.vector.quantize_mx(out=codes[:].bitcast(FP8X4), scales=plane[:], in_=values[:].rearrange("p v t -> p (v t)"))
+        def quantize(values, v0, v1, name):
+            codes = keep.tile([P, v1 - v0], U32, name=name + "_codes", align_bytes=64)
+            plane = keep.tile([P, v1 - v0], U8, name=name + "_plane", align_bytes=64)
+            nc.vector.quantize_mx(out=codes[:].bitcast(FP8X4), scales=plane[:], in_=values[:, v0:v1, :].rearrange("p v t -> p (v t)"))
             return codes, plane
 
-        pending = None
-        for t in range(PACK):
-            near = ring.tile([P, 4, V], BF16, name="near")
-            for d in range(4):
-                nc.vector.tensor_copy(near[:, d, :], h[t][:].indirect(pos_sb[d][:]))
-                if d == 0 and pending is not None:
-                    pending()
-            if t < 2:
-                nc.vector.tensor_copy(c_planes[:, t, :], h[t][:].indirect(cen_sb[:]))
-            if t < 3:
-                pair = ring.tile([P, 2, V], BF16, name="pair")
+        def centre_in_place(t):
+            nc.vector.tensor_copy(c_in[:, HALF:, t], h[t][:].indirect(entries(cen_sb, HALF, V)))
+
+        pair = None
+        for t in range(PACK + 1):
+            if t < PACK:
+                near = ring.tile([P, 4, V], BF16, name="near")
+                nc.vector.tensor_copy(near[:, 0, :], h[t][:].indirect(pos_sb[0][:]))
             else:
-                pair = keep.tile([P, 2, V], BF16, name="pair_last", tag="pair_last", align_bytes=64)
-            nc.vector.tensor_tensor(pair[:], near[:, 0:2, :], near[:, 2:4, :], MAX)
-
-            def finish(t=t, pair=pair):
-                nc.vector.tensor_tensor(z_planes[:, t, :], pair[:, 0, :], pair[:, 1, :], MAX)
-                if t == 1:
-                    weave(z_in[0], z_planes, 0, 0)
-                    weave(z_in[1], z_planes, 0, 1)
-                    weave(c_in[0], c_planes, 0, 0)
-
-            pending = finish
-        pending()
-        c_late = keep.tile([P, 2, HALF], BF16, name="c_late", tag="pair_last", align_bytes=64)
-        for t in (2, 3):
-            nc.vector.tensor_copy(c_late[:, t - 2, :], h[t][:].indirect(entries(cen_sb, 0, HALF)))
-        acc = []
-        for half in range(2):
-            weave(z_in[half], z_planes, 2, half)
-            codes, plane = quantize(z_in[half], "z%d" % half)
-            bank = psum_out.tile([P, HALF], F32, name="acc_out")
+                centre_in_place(2)
+            if t > 0:
+                nc.vector.tensor_tensor(z_planes[:, t - 1, :], pair[:, 0, :], pair[:, 1, :], MAX)
+            if t == 2:
+                weave(z_in, z_planes, 0, 0, V)
+                weave(c_in, c_planes, 0, 0, V)
+            if t < PACK:
+                for d in range(1, 4):
+                    nc.vector.tensor_copy(near[:, d, :], h[t][:].indirect(pos_sb[d][:]))
+                count = V if t < 2 else HALF
+                nc.vector.tensor_copy(c_planes[:, t, :count], h[t][:].indirect(entries(cen_sb, 0, count)))
+                if t == 3:
+                    weave(c_in, c_planes, 2, 0, HALF)
+                pair = ring.tile([P, 2, V], BF16, name="pair")
+                nc.vector.tensor_tensor(pair[:], near[:, 0:2, :], near[:, 2:4, :], MAX)
+        centre_in_place(3)
+        chunks = ((0, HALF), (HALF, V - 128), (V - 128, V))
+        for v0, v1 in chunks:
+            weave(z_in, z_planes, 2, v0, v1)
+        c_quantized = [quantize(c_in, v0, v0 + HALF, "c%d" % v0) for v0 in (0, HALF)]
+        acc_out = []
+        for v0, v1 in chunks:
+            codes, plane = c_quantized[v0 // HALF]
+            cols = slice(v0 % HALF, v0 % HALF + v1 - v0)
+            acc = psum_out.tile([P, v1 - v0], F32, name="acc_out")
             nc.tensor.matmul_mx(
-                out=bank[:], lhsT=w3_codes[:].bitcast(FP8X4), lhsT_scale=w3_plane[:],
-                rhs=codes[:].bitcast(FP8X4), rhs_scale=plane[:], start=True, stop=False,
+                out=acc[:], lhsT=w2_codes[:].bitcast(FP8X4), lhsT_scale=w2_plane[:],
+                rhs=codes[:, cols].bitcast(FP8X4), rhs_scale=plane[:, cols], start=True, stop=False,
             )
-            acc.append(bank)
-        nc.scalar.copy(c_in[0][:, :, 2:4], c_late[:].rearrange("p t v -> p v t"))
-        c_in.append(keep.tile([P, HALF, PACK], BF16, name="c_in1", tag="mx_in1", align_bytes=64))
-        weave(c_in[1], c_planes, 0, 1)
-        for t in (2, 3):
-            nc.vector.tensor_copy(c_in[1][:, :, t], h[t][:].indirect(entries(cen_sb, HALF, V)))
-        for half in range(2):
-            codes, plane = quantize(c_in[half], "c%d" % half)
+            acc_out.append(acc)
+        for acc, (v0, v1) in zip(acc_out, chunks):
+            codes, plane = quantize(z_in, v0, v1, "z%d" % v0)
             nc.tensor.matmul_mx(
-                out=acc[half][:], lhsT=w2_codes[:].bitcast(FP8X4), lhsT_scale=w2_plane[:],
+                out=acc[:], lhsT=w3_codes[:].bitcast(FP8X4), lhsT_scale=w3_plane[:],
                 rhs=codes[:].bitcast(FP8X4), rhs_scale=plane[:], start=False, stop=True,
             )
-            result = keep.tile([P, HALF], F32, name="result%d" % half)
-            nc.scalar.activation(result[:], acc[half][:], RELU)
-            nc.sync.dma_start(out=out[:, half * HALF : (half + 1) * HALF], in_=result[:])
+            result = keep.tile([P, v1 - v0], F32, name="result%d" % v0)
+            nc.scalar.activation(result[:], acc[:], RELU)
+            nc.scalar.dma_start(out=out[:, v0:v1], in_=result[:])

@@ -54,14 +54,14 @@ def tile_picked_sagecat_maxrelu_p_kernel(
         pos_sb = [lists.tile([P, V // LIST_ROWS], U16, name="pos_sb%d" % d) for d in range(4)]
         cen_sb = lists.tile([P, V // LIST_ROWS], U16, name="cen_sb")
         w1_rows = w1.rearrange("(p j) c -> p j c", j=PACK)
-        w1_parts = ((0, 256), (256, H))
-        w1_raw = [keep.tile([P, PACK, c1 - c0], F32, name="w1_raw%d" % c0) for c0, c1 in w1_parts]
-        nc.sync.dma_start(out=w1_raw[0][:], in_=w1_rows[:, :, :256])
+        w1_parts = ((0, 2), (2, 4))
+        w1_raw = [keep.tile([P, 2, H], F32, name="w1_raw%d" % j0) for j0, j1 in w1_parts]
+        nc.sync.dma_start(out=w1_raw[0][:], in_=w1_rows[:, 0:2, :])
         nc.sync.dma_start(offs_sb[:], offs)
         load_scale_rows(nc.sync, xs_all, x_scales)
         xw_all = keep.tile([P, T], I32, name="xw_all", align_bytes=64)
         nc.sync.dma_start(out=xw_all[:], in_=words_of(x_words))
-        nc.sync.dma_start(out=w1_raw[1][:], in_=w1_rows[:, :, 256:])
+        nc.sync.dma_start(out=w1_raw[1][:], in_=w1_rows[:, 2:4, :])
         nc.sync.dma_start(pos_sb[0][:], pos1)
         nc.sync.dma_start(pos_sb[1][:], pos2)
         nc.sync.dma_start(pos_sb[2][:], pos3)
@@ -86,10 +86,10 @@ def tile_picked_sagecat_maxrelu_p_kernel(
 
         w1_lead = keep.tile([P, 1, P, PACK], BF16, name="w1_lead", tag="w1_then_x", align_bytes=64)
         w1_rest = keep.tile([P, PACK - 1, P, PACK], BF16, name="w1_rest", align_bytes=64)
-        for raw, (c0, c1) in zip(w1_raw, w1_parts):
+        for raw, (j0, j1) in zip(w1_raw, w1_parts):
             by_plane = raw[:].rearrange("p j (m t) -> p m t j", t=PACK)
             for grouped, t0, t1 in ((w1_lead, 0, 1), (w1_rest, 1, PACK)):
-                nc.scalar.copy(grouped[:, :, c0 // PACK : c1 // PACK, :].rearrange("p t m j -> p m t j"), by_plane[:, :, t0:t1, :])
+                nc.scalar.copy(grouped[:, :, :, j0:j1].rearrange("p t m j -> p m t j"), by_plane[:, :, t0:t1, :])
         w1_codes = keep.tile([P, H], U32, name="w1_codes", align_bytes=64)
         w1_plane = keep.tile([P, H], U8, name="w1_plane", align_bytes=64)
 

@@ -14,6 +14,8 @@ U8 = mybir.dt.uint8
 FP8X4 = mybir.dt.float8_e4m3fn_x4
 RELU = mybir.ActivationFunctionType.Relu
 MAX = mybir.AluOpType.max
+ADD = mybir.AluOpType.add
+SUB = mybir.AluOpType.subtract
 
 P = 128
 PACK = 4
@@ -21,6 +23,7 @@ BANK = 512
 LIST_ROWS = 16
 LAST = 256
 HALF = V // 2
+EARLY = V - 128
 
 
 def load_scale_rows(queue, plane, scales):
@@ -43,7 +46,7 @@ def tile_picked_sagecat_maxrelu_p_kernel(
     with ExitStack() as ctx:
         lists = ctx.enter_context(tc.tile_pool(name="lists", bufs=1))
         keep = ctx.enter_context(tc.tile_pool(name="keep", bufs=1))
-        ring = ctx.enter_context(tc.tile_pool(name="ring", bufs=2))
+        shared = ctx.enter_context(tc.tile_pool(name="shared", bufs=1))
         psum_h = ctx.enter_context(tc.psum_pool(name="psum_h", bufs=5))
         psum_out = ctx.enter_context(tc.psum_pool(name="psum_out", bufs=3))
 
@@ -124,10 +127,15 @@ def tile_picked_sagecat_maxrelu_p_kernel(
         z_planes = keep.tile([P, PACK, V], BF16, name="z_planes", align_bytes=64)
         c_planes = keep.tile([P, PACK, V], BF16, name="c_planes", align_bytes=64)
         z_in = keep.tile([P, V, PACK], BF16, name="z_in", align_bytes=64)
-        c_in = keep.tile([P, V, PACK], BF16, name="c_in", align_bytes=64)
 
-        def weave(dst, planes, t0, v0, v1):
-            nc.scalar.copy(dst[:, v0:v1, t0 : t0 + 2], planes[:, t0 : t0 + 2, v0:v1].rearrange("p t v -> p v t"))
+        def gather_near(dst, t, v0, v1):
+            for d in range(4):
+                nc.vector.tensor_copy(dst[:, d, :], h[t][:].indirect(entries(pos_sb[d], v0, v1)))
+
+        def weave(dst, planes, v0, v1):
+            nc.scalar.copy(
+                dst[:, v0:v1, :].rearrange("p (c i) t -> p c t i", i=4), planes[:, :, v0:v1].rearrange("p t (c i) -> p c t i", i=4)
+            )
 
         def quantize(values, v0, v1, name):
             codes = keep.tile([P, v1 - v0], U32, name=name + "_codes", align_bytes=64)
@@ -135,35 +143,67 @@ def tile_picked_sagecat_maxrelu_p_kernel(
             nc.vector.quantize_mx(out=codes[:].bitcast(FP8X4), scales=plane[:], in_=values[:, v0:v1, :].rearrange("p v t -> p (v t)"))
             return codes, plane
 
-        def centre_in_place(t):
-            nc.vector.tensor_copy(c_in[:, HALF:, t], h[t][:].indirect(entries(cen_sb, HALF, V)))
+        near = [keep.tile([P, 4, V], BF16, name="near%d" % t) for t in range(3)]
+        near3_early = keep.tile([P, 4, EARLY], BF16, name="near3_early")
+        gather_near(near[0], 0, 0, V)
+        gather_near(near[1], 1, 0, V)
+        for t in range(PACK):
+            nc.vector.tensor_copy(c_planes[:, t, :], h[t][:].indirect(cen_sb[:]))
+        gather_near(near[2], 2, 0, V)
+        gather_near(near3_early, 3, 0, EARLY)
 
-        pair = None
-        for t in range(PACK + 1):
-            if t < PACK:
-                near = ring.tile([P, 4, V], BF16, name="near")
-                nc.vector.tensor_copy(near[:, 0, :], h[t][:].indirect(pos_sb[0][:]))
-            else:
-                centre_in_place(2)
-            if t > 0:
-                nc.vector.tensor_tensor(z_planes[:, t - 1, :], pair[:, 0, :], pair[:, 1, :], MAX)
-            if t == 2:
-                weave(z_in, z_planes, 0, 0, V)
-                weave(c_in, c_planes, 0, 0, V)
-            if t < PACK:
-                for d in range(1, 4):
-                    nc.vector.tensor_copy(near[:, d, :], h[t][:].indirect(pos_sb[d][:]))
-                count = V if t < 2 else HALF
-                nc.vector.tensor_copy(c_planes[:, t, :count], h[t][:].indirect(entries(cen_sb, 0, count)))
-                if t == 3:
-                    weave(c_in, c_planes, 2, 0, HALF)
-                pair = ring.tile([P, 2, V], BF16, name="pair")
-                nc.vector.tensor_tensor(pair[:], near[:, 0:2, :], near[:, 2:4, :], MAX)
-        centre_in_place(3)
-        chunks = ((0, HALF), (HALF, V - 128), (V - 128, V))
-        for v0, v1 in chunks:
-            weave(z_in, z_planes, 2, v0, v1)
-        c_quantized = [quantize(c_in, v0, v0 + HALF, "c%d" % v0) for v0 in (0, HALF)]
+        def excess(a, b, diff, over):
+            nc.gpsimd.tensor_tensor(diff[:], a, b, SUB)
+            nc.scalar.activation(over[:], diff[:], RELU)
+
+        diffs = [keep.tile([P, V], F32, name="diff%d" % n) for n in range(5)] + [shared.tile([P, V], F32, name="diff5", offset=0, align_bytes=64)]
+        overs = [keep.tile([P, V], F32, name="over%d" % n) for n in range(5)] + [shared.tile([P, V], F32, name="over5", offset=4096, align_bytes=64)]
+        pairs = [keep.tile([P, 2, V], BF16, name="pair0"), shared.tile([P, 2, V], BF16, name="pair1", offset=6144, align_bytes=64)]
+
+        def start_pair(t, d):
+            excess(near[t][:, 2 * d, :], near[t][:, 2 * d + 1, :], diffs[3 * t + d], overs[3 * t + d])
+
+        def finish_pair(t, d):
+            nc.gpsimd.tensor_tensor(pairs[t][:, d, :], near[t][:, 2 * d + 1, :], overs[3 * t + d][:], ADD)
+
+        def start_slab(t):
+            excess(pairs[t][:, 0, :], pairs[t][:, 1, :], diffs[3 * t + 2], overs[3 * t + 2])
+
+        def finish_slab(t):
+            nc.gpsimd.tensor_tensor(z_planes[:, t, :], pairs[t][:, 1, :], overs[3 * t + 2][:], ADD)
+
+        start_pair(0, 0)
+        start_pair(0, 1)
+        finish_pair(0, 0)
+        finish_pair(0, 1)
+        start_pair(1, 0)
+        start_slab(0)
+        start_pair(1, 1)
+        finish_slab(0)
+        finish_pair(1, 0)
+        finish_pair(1, 1)
+        start_slab(1)
+        finish_slab(1)
+
+        c_in = shared.tile([P, V, PACK], BF16, name="c_in", offset=0, align_bytes=64)
+        weave(c_in, c_planes, 0, V)
+        pair2 = shared.tile([P, 2, V], BF16, name="pair2", offset=4096, align_bytes=64)
+        pair3_early = shared.tile([P, 2, EARLY], BF16, name="pair3_early", offset=6144, align_bytes=64)
+        near3_late = shared.tile([P, 4, V - EARLY], BF16, name="near3_late", offset=7680, align_bytes=64)
+        pair3_late = keep.tile([P, 2, V - EARLY], BF16, name="pair3_late")
+        nc.vector.tensor_tensor(pair2[:], near[2][:, 0:2, :], near[2][:, 2:4, :], MAX)
+        nc.vector.tensor_tensor(pair3_early[:], near3_early[:, 0:2, :], near3_early[:, 2:4, :], MAX)
+        nc.vector.tensor_tensor(z_planes[:, 2, :], pair2[:, 0, :], pair2[:, 1, :], MAX)
+        nc.vector.tensor_tensor(z_planes[:, 3, :EARLY], pair3_early[:, 0, :], pair3_early[:, 1, :], MAX)
+        chunks = ((0, HALF), (HALF, EARLY), (EARLY, V))
+        for v0, v1 in chunks[:2]:
+            weave(z_in, z_planes, v0, v1)
+        gather_near(near3_late, 3, EARLY, V)
+        c_quantized = [quantize(c_in, 0, HALF, "c0")]
+        nc.vector.tensor_tensor(pair3_late[:], near3_late[:, 0:2, :], near3_late[:, 2:4, :], MAX)
+        c_quantized.append(quantize(c_in, HALF, V, "c1"))
+        nc.vector.tensor_tensor(z_planes[:, 3, EARLY:], pair3_late[:, 0, :], pair3_late[:, 1, :], MAX)
+        weave(z_in, z_planes, EARLY, V)
         acc_out = []
         for v0, v1 in chunks:
             codes, plane = c_quantized[v0 // HALF]

@@ -14,6 +14,7 @@ U8 = mybir.dt.uint8
 FP8X4 = mybir.dt.float8_e4m3fn_x4
 RELU = mybir.ActivationFunctionType.Relu
 MAX = mybir.AluOpType.max
+MULT = mybir.AluOpType.mult
 ADD = mybir.AluOpType.add
 SUB = mybir.AluOpType.subtract
 
@@ -89,10 +90,14 @@ def tile_picked_sagecat_maxrelu_p_kernel(
 
         w1_lead = keep.tile([P, 1, P, PACK], BF16, name="w1_lead", tag="w1_then_x", align_bytes=64)
         w1_rest = keep.tile([P, PACK - 1, P, PACK], BF16, name="w1_rest", align_bytes=64)
-        for raw, (j0, j1) in zip(w1_raw, w1_parts):
-            by_plane = raw[:].rearrange("p j (m t) -> p m t j", t=PACK)
-            for grouped, t0, t1 in ((w1_lead, 0, 1), (w1_rest, 1, PACK)):
-                nc.scalar.copy(grouped[:, :, :, j0:j1].rearrange("p t m j -> p m t j"), by_plane[:, :, t0:t1, :])
+        early_rows, late_rows = [raw[:].rearrange("p j (m t) -> p m t j", t=PACK) for raw in w1_raw]
+        lead_view = w1_lead[:].rearrange("p t m j -> p m t j")
+        rest_view = w1_rest[:].rearrange("p t m j -> p m t j")
+        nc.scalar.copy(lead_view[:, :, :, 0:2], early_rows[:, :, 0:1, :])
+        nc.scalar.copy(rest_view[:, :, :, 0:2], early_rows[:, :, 1:4, :])
+        nc.scalar.copy(lead_view[:, :, :, 2:4], late_rows[:, :, 0:1, :])
+        nc.scalar.copy(rest_view[:, :, 0:2, 2:4], late_rows[:, :, 1:3, :])
+        nc.gpsimd.tensor_scalar(rest_view[:, :, 2, 2:4], late_rows[:, :, 3, :], 1.0, 0.0, MULT, ADD)
         w1_codes = keep.tile([P, H], U32, name="w1_codes", align_bytes=64)
         w1_plane = keep.tile([P, H], U8, name="w1_plane", align_bytes=64)
 
@@ -105,24 +110,33 @@ def tile_picked_sagecat_maxrelu_p_kernel(
         nc.vector.tensor_copy(xw_late[:], xw_window.indirect(entries(offs_sb, S - LAST, S)))
         quantize_w1(1, 2, w1_rest[:, 0:1])
         quantize_w1(2, 4, w1_rest[:, 1:3])
-        pieces = ((xw_early[:, :BANK], 0, BANK), (xw_early[:, BANK:], BANK, LAST), (xw_late[:], S - LAST, LAST))
-        h = []
-        for t in range(PACK):
-            h_t = keep.tile([P, S], F32, name="h%d" % t, align_bytes=64)
-            banks = [psum_h.tile([P, BANK], F32, name="acc_h") for bank in range(3 if t == 0 else 2)]
-            for number, (words, first, count) in enumerate(pieces):
-                acc = banks[number][:, :count] if t == 0 or number == 0 else banks[1][:, first - BANK : first - BANK + count]
-                nc.tensor.matmul_mx(
-                    out=acc, lhsT=w1_codes[:, t * P : (t + 1) * P].bitcast(FP8X4), lhsT_scale=w1_plane[:, t * P : (t + 1) * P],
-                    rhs=words.bitcast(FP8X4), rhs_scale=xs_pick[:, first : first + count], start=True, stop=True,
-                )
-                if t == 0 and number == 2:
-                    nc.vector.tensor_scalar_max(h_t[:, first : first + count], acc, 0.0)
-                elif t == 0 or number == 0:
-                    nc.scalar.activation(h_t[:, first : first + count], acc, RELU)
-                elif number == 2:
-                    nc.scalar.activation(h_t[:, BANK:], banks[1][:], RELU)
-            h.append(h_t)
+        def picked(first, count):
+            return xw_early[:, first : first + count] if first < S - LAST else xw_late[:, first - (S - LAST) : first - (S - LAST) + count]
+
+        def multiply_w1(acc, t, first, count):
+            nc.tensor.matmul_mx(
+                out=acc, lhsT=w1_codes[:, t * P : (t + 1) * P].bitcast(FP8X4), lhsT_scale=w1_plane[:, t * P : (t + 1) * P],
+                rhs=picked(first, count).bitcast(FP8X4), rhs_scale=xs_pick[:, first : first + count], start=True, stop=True,
+            )
+
+        h = [keep.tile([P, S], F32, name="h%d" % t, align_bytes=64) for t in range(PACK)]
+        first = 0
+        for number, count in enumerate((256, 256, 256, 128, 128)):
+            bank = psum_h.tile([P, BANK], F32, name="acc_h")
+            multiply_w1(bank[:, :count], 0, first, count)
+            if number % 2 == 0:
+                nc.scalar.activation(h[0][:, first : first + count], bank[:, :count], RELU)
+            else:
+                nc.vector.tensor_scalar_max(h[0][:, first : first + count], bank[:, :count], 0.0)
+            first = first + count
+        for t in range(1, PACK):
+            low = psum_h.tile([P, BANK], F32, name="acc_h")
+            multiply_w1(low[:], t, 0, BANK)
+            nc.scalar.activation(h[t][:, :BANK], low[:], RELU)
+            high = psum_h.tile([P, BANK], F32, name="acc_h")
+            multiply_w1(high[:, :LAST], t, BANK, LAST)
+            multiply_w1(high[:, LAST:], t, S - LAST, LAST)
+            nc.scalar.activation(h[t][:, BANK:], high[:], RELU)
 
         z_planes = keep.tile([P, PACK, V], BF16, name="z_planes", align_bytes=64)
         c_planes = keep.tile([P, PACK, V], BF16, name="c_planes", align_bytes=64)
@@ -132,9 +146,9 @@ def tile_picked_sagecat_maxrelu_p_kernel(
             for d in range(4):
                 nc.vector.tensor_copy(dst[:, d, :], h[t][:].indirect(entries(pos_sb[d], v0, v1)))
 
-        def weave(dst, planes, v0, v1):
+        def weave(dst, planes, t0, t1, v0, v1):
             nc.scalar.copy(
-                dst[:, v0:v1, :].rearrange("p (c i) t -> p c t i", i=4), planes[:, :, v0:v1].rearrange("p t (c i) -> p c t i", i=4)
+                dst[:, v0:v1, t0:t1].rearrange("p (c i) t -> p c t i", i=4), planes[:, t0:t1, v0:v1].rearrange("p t (c i) -> p c t i", i=4)
             )
 
         def quantize(values, v0, v1, name):
@@ -156,9 +170,14 @@ def tile_picked_sagecat_maxrelu_p_kernel(
             nc.gpsimd.tensor_tensor(diff[:], a, b, SUB)
             nc.scalar.activation(over[:], diff[:], RELU)
 
-        diffs = [keep.tile([P, V], F32, name="diff%d" % n) for n in range(5)] + [shared.tile([P, V], F32, name="diff5", offset=0, align_bytes=64)]
-        overs = [keep.tile([P, V], F32, name="over%d" % n) for n in range(5)] + [shared.tile([P, V], F32, name="over5", offset=4096, align_bytes=64)]
-        pairs = [keep.tile([P, 2, V], BF16, name="pair0"), shared.tile([P, 2, V], BF16, name="pair1", offset=6144, align_bytes=64)]
+        def shared_row(name, offset):
+            return shared.tile([P, V], F32, name=name, offset=offset, align_bytes=64)
+
+        diffs = [keep.tile([P, V], F32, name="diff%d" % n) for n in range(3)]
+        diffs = diffs + [shared_row("diff3", 0), shared_row("diff4", 2048), shared_row("diff5", 6144), shared_row("diff6", 4096)]
+        overs = [shared_row("over0", 0), shared_row("over1", 2048)] + [keep.tile([P, V], F32, name="over%d" % n) for n in (2, 3)]
+        overs = overs + [shared_row("over4", 4096), keep.tile([P, V], F32, name="over5"), shared_row("over6", 9472)]
+        pairs = [keep.tile([P, 2, V], BF16, name="pair%d" % t) for t in range(2)] + [keep.tile([P, 1, V], BF16, name="pair2")]
 
         def start_pair(t, d):
             excess(near[t][:, 2 * d, :], near[t][:, 2 * d + 1, :], diffs[3 * t + d], overs[3 * t + d])
@@ -183,27 +202,31 @@ def tile_picked_sagecat_maxrelu_p_kernel(
         finish_pair(1, 0)
         finish_pair(1, 1)
         start_slab(1)
+        start_pair(2, 0)
         finish_slab(1)
+        finish_pair(2, 0)
 
-        c_in = shared.tile([P, V, PACK], BF16, name="c_in", offset=0, align_bytes=64)
-        weave(c_in, c_planes, 0, V)
-        pair2 = shared.tile([P, 2, V], BF16, name="pair2", offset=4096, align_bytes=64)
-        pair3_early = shared.tile([P, 2, EARLY], BF16, name="pair3_early", offset=6144, align_bytes=64)
-        near3_late = shared.tile([P, 4, V - EARLY], BF16, name="near3_late", offset=7680, align_bytes=64)
+        c_in = [shared.tile([P, HALF, PACK], BF16, name="c_in%d" % n, offset=offset, align_bytes=64) for n, offset in enumerate((6144, 4096))]
+        for n in range(2):
+            weave(c_in[n], c_planes[:, :, n * HALF : (n + 1) * HALF], 0, PACK, 0, HALF)
+        weave(z_in, z_planes, 0, 2, 0, V)
+        pair3_early = shared.tile([P, 2, EARLY], BF16, name="pair3_early", offset=8192, align_bytes=64)
+        pair2_second = shared.tile([P, V], BF16, name="pair2_second", offset=9728, align_bytes=64)
+        near3_late = shared.tile([P, 4, V - EARLY], BF16, name="near3_late", offset=10752, align_bytes=64)
         pair3_late = keep.tile([P, 2, V - EARLY], BF16, name="pair3_late")
-        nc.vector.tensor_tensor(pair2[:], near[2][:, 0:2, :], near[2][:, 2:4, :], MAX)
+        nc.vector.tensor_tensor(pair2_second[:], near[2][:, 2, :], near[2][:, 3, :], MAX)
         nc.vector.tensor_tensor(pair3_early[:], near3_early[:, 0:2, :], near3_early[:, 2:4, :], MAX)
-        nc.vector.tensor_tensor(z_planes[:, 2, :], pair2[:, 0, :], pair2[:, 1, :], MAX)
+        nc.vector.tensor_tensor(z_planes[:, 2, :], pairs[2][:, 0, :], pair2_second[:], MAX)
         nc.vector.tensor_tensor(z_planes[:, 3, :EARLY], pair3_early[:, 0, :], pair3_early[:, 1, :], MAX)
         chunks = ((0, HALF), (HALF, EARLY), (EARLY, V))
         for v0, v1 in chunks[:2]:
-            weave(z_in, z_planes, v0, v1)
+            weave(z_in, z_planes, 2, PACK, v0, v1)
         gather_near(near3_late, 3, EARLY, V)
-        c_quantized = [quantize(c_in, 0, HALF, "c0")]
+        c_quantized = [quantize(c_in[0], 0, HALF, "c0")]
         nc.vector.tensor_tensor(pair3_late[:], near3_late[:, 0:2, :], near3_late[:, 2:4, :], MAX)
-        c_quantized.append(quantize(c_in, HALF, V, "c1"))
+        c_quantized.append(quantize(c_in[1], 0, HALF, "c1"))
         nc.vector.tensor_tensor(z_planes[:, 3, EARLY:], pair3_late[:, 0, :], pair3_late[:, 1, :], MAX)
-        weave(z_in, z_planes, EARLY, V)
+        weave(z_in, z_planes, 2, PACK, EARLY, V)
         acc_out = []
         for v0, v1 in chunks:
             codes, plane = c_quantized[v0 // HALF]
@@ -221,5 +244,8 @@ def tile_picked_sagecat_maxrelu_p_kernel(
                 rhs=codes[:].bitcast(FP8X4), rhs_scale=plane[:], start=False, stop=True,
             )
             result = keep.tile([P, v1 - v0], F32, name="result%d" % v0)
-            nc.scalar.activation(result[:], acc[:], RELU)
-            nc.scalar.dma_start(out=out[:, v0:v1], in_=result[:])
+            if v1 == V:
+                nc.vector.tensor_scalar_max(result[:], acc[:], 0.0)
+            else:
+                nc.scalar.activation(result[:], acc[:], RELU)
+            nc.sync.dma_start(out=out[:, v0:v1], in_=result[:])

@@ -95,9 +95,9 @@ def tile_picked_sagecat_maxrelu_p_kernel(
         rest_view = w1_rest[:].rearrange("p t m j -> p m t j")
         nc.scalar.copy(lead_view[:, :, :, 0:2], early_rows[:, :, 0:1, :])
         nc.scalar.copy(rest_view[:, :, :, 0:2], early_rows[:, :, 1:4, :])
-        nc.scalar.copy(lead_view[:, :, :, 2:4], late_rows[:, :, 0:1, :])
-        nc.scalar.copy(rest_view[:, :, 0:2, 2:4], late_rows[:, :, 1:3, :])
-        nc.gpsimd.tensor_scalar(rest_view[:, :, 2, 2:4], late_rows[:, :, 3, :], 1.0, 0.0, MULT, ADD)
+        nc.scalar.copy(lead_view[:, : P // 2, 0, 2:4], late_rows[:, : P // 2, 0, :])
+        nc.gpsimd.tensor_scalar(lead_view[:, P // 2 :, 0, 2:4], late_rows[:, P // 2 :, 0, :], 1.0, 0.0, MULT, ADD)
+        nc.scalar.copy(rest_view[:, :, :, 2:4], late_rows[:, :, 1:4, :])
         w1_codes = keep.tile([P, H], U32, name="w1_codes", align_bytes=64)
         w1_plane = keep.tile([P, H], U8, name="w1_plane", align_bytes=64)
 
@@ -124,7 +124,7 @@ def tile_picked_sagecat_maxrelu_p_kernel(
         for number, count in enumerate((256, 256, 256, 128, 128)):
             bank = psum_h.tile([P, BANK], F32, name="acc_h")
             multiply_w1(bank[:, :count], 0, first, count)
-            if number % 2 == 0:
+            if number in (1, 2, 4):
                 nc.scalar.activation(h[0][:, first : first + count], bank[:, :count], RELU)
             else:
                 nc.vector.tensor_scalar_max(h[0][:, first : first + count], bank[:, :count], 0.0)
@@ -174,9 +174,10 @@ def tile_picked_sagecat_maxrelu_p_kernel(
             return shared.tile([P, V], F32, name=name, offset=offset, align_bytes=64)
 
         diffs = [keep.tile([P, V], F32, name="diff%d" % n) for n in range(3)]
-        diffs = diffs + [shared_row("diff3", 0), shared_row("diff4", 2048), shared_row("diff5", 6144), shared_row("diff6", 4096)]
-        overs = [shared_row("over0", 0), shared_row("over1", 2048)] + [keep.tile([P, V], F32, name="over%d" % n) for n in (2, 3)]
-        overs = overs + [shared_row("over4", 4096), keep.tile([P, V], F32, name="over5"), shared_row("over6", 9472)]
+        diffs = diffs + [shared_row("diff3", 0), shared_row("diff4", 2048), shared_row("diff5", 6144), shared_row("diff6", 12288)]
+        both_overs = shared.tile([P, 2, V], F32, name="both_overs", offset=12288, align_bytes=64)
+        overs = [shared_row("over0", 0), shared_row("over1", 2048), keep.tile([P, V], F32, name="over2"), both_overs[:, 0, :], both_overs[:, 1, :]]
+        overs = overs + [keep.tile([P, V], F32, name="over5"), shared_row("over6", 9472)]
         pairs = [keep.tile([P, 2, V], BF16, name="pair%d" % t) for t in range(2)] + [keep.tile([P, 1, V], BF16, name="pair2")]
 
         def start_pair(t, d):
@@ -199,14 +200,13 @@ def tile_picked_sagecat_maxrelu_p_kernel(
         start_slab(0)
         start_pair(1, 1)
         finish_slab(0)
-        finish_pair(1, 0)
-        finish_pair(1, 1)
+        nc.gpsimd.tensor_tensor(pairs[1][:], near[1][:, 1:4:2, :], both_overs[:], ADD)
         start_slab(1)
         start_pair(2, 0)
         finish_slab(1)
         finish_pair(2, 0)
 
-        c_in = [shared.tile([P, HALF, PACK], BF16, name="c_in%d" % n, offset=offset, align_bytes=64) for n, offset in enumerate((6144, 4096))]
+        c_in = [shared.tile([P, HALF, PACK], BF16, name="c_in%d" % n, offset=offset, align_bytes=64) for n, offset in enumerate((6144, 12288))]
         for n in range(2):
             weave(c_in[n], c_planes[:, :, n * HALF : (n + 1) * HALF], 0, PACK, 0, HALF)
         weave(z_in, z_planes, 0, 2, 0, V)

@@ -20,16 +20,18 @@ SUB = mybir.AluOpType.subtract
 
 P = 128
 PACK = 4
+QUADRANT = 32
 BANK = 512
 LIST_ROWS = 16
-LAST = 256
+NEIGHBOURS = 4
+LATE_WORDS = 256
 HALF = V // 2
 EARLY = V - 128
 
 
-def load_scale_rows(queue, plane, scales):
-    for q in range(4):
-        queue.dma_start(out=plane[32 * q : 32 * q + 4, :].bitcast(I32), in_=scales[0, 4 * q : 4 * q + 4, :].bitcast(I32))
+def load_scale_rows(nc, plane, scales):
+    for r in range(PACK):
+        nc.sync.dma_start(out=plane[r:P:QUADRANT, :].bitcast(I32), in_=scales[0, r : PACK * PACK : PACK, :].bitcast(I32))
 
 
 def words_of(dram_words):
@@ -47,7 +49,7 @@ def tile_picked_sagecat_maxrelu_p_kernel(
     with ExitStack() as ctx:
         lists = ctx.enter_context(tc.tile_pool(name="lists", bufs=1))
         keep = ctx.enter_context(tc.tile_pool(name="keep", bufs=1))
-        shared = ctx.enter_context(tc.tile_pool(name="shared", bufs=1))
+        after_gpsimd = ctx.enter_context(tc.tile_pool(name="after_gpsimd", bufs=1))
         psum_h = ctx.enter_context(tc.psum_pool(name="psum_h", bufs=5))
         psum_out = ctx.enter_context(tc.psum_pool(name="psum_out", bufs=3))
 
@@ -55,21 +57,20 @@ def tile_picked_sagecat_maxrelu_p_kernel(
         nc.vector.memset(xs_all[:, : T // 2].bitcast(I32), 0)
         nc.gpsimd.memset(xs_all[:, T // 2 :].bitcast(I32), 0)
         offs_sb = lists.tile([P, S // LIST_ROWS], U16, name="offs_sb")
-        pos_sb = [lists.tile([P, V // LIST_ROWS], U16, name="pos_sb%d" % d) for d in range(4)]
+        pos_sb = [lists.tile([P, V // LIST_ROWS], U16, name="pos_sb%d" % d) for d in range(NEIGHBOURS)]
         cen_sb = lists.tile([P, V // LIST_ROWS], U16, name="cen_sb")
         w1_rows = w1.rearrange("(p j) c -> p j c", j=PACK)
-        w1_parts = ((0, 2), (2, 4))
-        w1_raw = [keep.tile([P, 2, H], F32, name="w1_raw%d" % j0) for j0, j1 in w1_parts]
-        nc.sync.dma_start(out=w1_raw[0][:], in_=w1_rows[:, 0:2, :])
-        nc.sync.dma_start(offs_sb[:], offs)
-        load_scale_rows(nc.sync, xs_all, x_scales)
+        w1_early = keep.tile([P, 2, H], F32, name="w1_early")
+        w1_late = keep.tile([P, 2, H], F32, name="w1_late")
         xw_all = keep.tile([P, T], I32, name="xw_all", align_bytes=64)
+        nc.sync.dma_start(out=w1_early[:, 0, :], in_=w1_rows[:, 0, :])
+        nc.sync.dma_start(offs_sb[:], offs)
+        load_scale_rows(nc, xs_all, x_scales)
+        nc.sync.dma_start(out=w1_early[:, 1, :], in_=w1_rows[:, 1, :])
         nc.sync.dma_start(out=xw_all[:], in_=words_of(x_words))
-        nc.sync.dma_start(out=w1_raw[1][:], in_=w1_rows[:, 2:4, :])
-        nc.sync.dma_start(pos_sb[0][:], pos1)
-        nc.sync.dma_start(pos_sb[1][:], pos2)
-        nc.sync.dma_start(pos_sb[2][:], pos3)
-        nc.sync.dma_start(pos_sb[3][:], pos4)
+        nc.sync.dma_start(out=w1_late[:], in_=w1_rows[:, 2:4, :])
+        for offsets, pos in zip(pos_sb, (pos1, pos2, pos3, pos4)):
+            nc.sync.dma_start(offsets[:], pos)
         nc.sync.dma_start(cen_sb[:], cen)
 
         w2_codes = keep.tile([P, N], I32, name="w2_codes", align_bytes=64)
@@ -79,154 +80,149 @@ def tile_picked_sagecat_maxrelu_p_kernel(
         for codes, plane, words, scales in ((w3_codes, w3_plane, w3_words, w3_scales), (w2_codes, w2_plane, w2_words, w2_scales)):
             nc.sync.dma_start(out=codes[:], in_=words_of(words))
             nc.gpsimd.memset(plane[:].bitcast(I32), 0)
-            load_scale_rows(nc.sync, plane, scales)
+            load_scale_rows(nc, plane, scales)
 
         xs_pick = keep.tile([P, S], U8, name="xs_pick", align_bytes=64)
         nc.vector.tensor_copy(xs_pick[:], xs_all[:].indirect(offs_sb[:]))
         xw_window = xw_all[:].bitcast(U32)
-        xw_early = keep.tile([P, S - LAST], U32, name="xw_early", align_bytes=64)
-        for first, last in ((0, BANK), (BANK, S - LAST)):
+        early_words = S - LATE_WORDS
+        xw_early = keep.tile([P, early_words], U32, name="xw_early", align_bytes=64)
+        for first, last in ((0, BANK), (BANK, early_words)):
             nc.vector.tensor_copy(xw_early[:, first:last], xw_window.indirect(entries(offs_sb, first, last)))
 
-        w1_lead = keep.tile([P, 1, P, PACK], BF16, name="w1_lead", tag="w1_then_x", align_bytes=64)
-        w1_rest = keep.tile([P, PACK - 1, P, PACK], BF16, name="w1_rest", align_bytes=64)
-        early_rows, late_rows = [raw[:].rearrange("p j (m t) -> p m t j", t=PACK) for raw in w1_raw]
-        lead_view = w1_lead[:].rearrange("p t m j -> p m t j")
-        rest_view = w1_rest[:].rearrange("p t m j -> p m t j")
-        nc.scalar.copy(lead_view[:, :, :, 0:2], early_rows[:, :, 0:1, :])
-        nc.scalar.copy(rest_view[:, :, :, 0:2], early_rows[:, :, 1:4, :])
-        nc.scalar.copy(lead_view[:, : P // 2, 0, 2:4], late_rows[:, : P // 2, 0, :])
-        nc.gpsimd.tensor_scalar(lead_view[:, P // 2 :, 0, 2:4], late_rows[:, P // 2 :, 0, :], 1.0, 0.0, MULT, ADD)
-        nc.scalar.copy(rest_view[:, :, :, 2:4], late_rows[:, :, 1:4, :])
+        w1_slab0 = keep.tile([P, P, PACK], BF16, name="w1_slab0", tag="w1_slab0_then_late_words", align_bytes=64)
+        w1_others = keep.tile([P, PACK - 1, P, PACK], BF16, name="w1_others", align_bytes=64)
+        early_rows, late_rows = [raw[:].rearrange("p j (m t) -> p m t j", t=PACK) for raw in (w1_early, w1_late)]
+        others_by_place = w1_others[:].rearrange("p t m j -> p m t j")
+        for j in range(2):
+            nc.scalar.copy(w1_slab0[:, :, j], early_rows[:, :, 0, j])
+        nc.scalar.copy(others_by_place[:, :, :, 0:2], early_rows[:, :, 1:PACK, :])
+        nc.scalar.copy(w1_slab0[:, : P // 2, 2:4], late_rows[:, : P // 2, 0, :])
+        nc.gpsimd.tensor_scalar(w1_slab0[:, P // 2 :, 2:4], late_rows[:, P // 2 :, 0, :], 1.0, 0.0, MULT, ADD)
+        nc.scalar.copy(others_by_place[:, :, :, 2:4], late_rows[:, :, 1:PACK, :])
         w1_codes = keep.tile([P, H], U32, name="w1_codes", align_bytes=64)
         w1_plane = keep.tile([P, H], U8, name="w1_plane", align_bytes=64)
 
-        def quantize_w1(t0, t1, grouped):
+        def quantize_w1(t0, t1, values):
             cols = slice(t0 * P, t1 * P)
-            nc.vector.quantize_mx(out=w1_codes[:, cols].bitcast(FP8X4), scales=w1_plane[:, cols], in_=grouped.rearrange("p t m j -> p (t m j)"))
+            nc.vector.quantize_mx(out=w1_codes[:, cols].bitcast(FP8X4), scales=w1_plane[:, cols], in_=values)
 
-        quantize_w1(0, 1, w1_lead[:])
-        xw_late = keep.tile([P, LAST], U32, name="xw_late", tag="w1_then_x", align_bytes=64)
-        nc.vector.tensor_copy(xw_late[:], xw_window.indirect(entries(offs_sb, S - LAST, S)))
-        quantize_w1(1, 2, w1_rest[:, 0:1])
-        quantize_w1(2, 4, w1_rest[:, 1:3])
-        def picked(first, count):
-            return xw_early[:, first : first + count] if first < S - LAST else xw_late[:, first - (S - LAST) : first - (S - LAST) + count]
+        quantize_w1(0, 1, w1_slab0[:].rearrange("p m j -> p (m j)"))
+        xw_late = keep.tile([P, LATE_WORDS], U32, name="xw_late", tag="w1_slab0_then_late_words", align_bytes=64)
+        nc.vector.tensor_copy(xw_late[:], xw_window.indirect(entries(offs_sb, early_words, S)))
+        quantize_w1(1, 2, w1_others[:, 0:1].rearrange("p t m j -> p (t m j)"))
+        quantize_w1(2, 4, w1_others[:, 1:3].rearrange("p t m j -> p (t m j)"))
 
         def multiply_w1(acc, t, first, count):
+            if first < early_words:
+                words = xw_early[:, first : first + count]
+            else:
+                words = xw_late[:, first - early_words : first - early_words + count]
             nc.tensor.matmul_mx(
                 out=acc, lhsT=w1_codes[:, t * P : (t + 1) * P].bitcast(FP8X4), lhsT_scale=w1_plane[:, t * P : (t + 1) * P],
-                rhs=picked(first, count).bitcast(FP8X4), rhs_scale=xs_pick[:, first : first + count], start=True, stop=True,
+                rhs=words.bitcast(FP8X4), rhs_scale=xs_pick[:, first : first + count], start=True, stop=True,
             )
 
         h = [keep.tile([P, S], F32, name="h%d" % t, align_bytes=64) for t in range(PACK)]
-        first = 0
-        for number, count in enumerate((256, 256, 256, 128, 128)):
-            bank = psum_h.tile([P, BANK], F32, name="acc_h")
-            multiply_w1(bank[:, :count], 0, first, count)
-            if number in (1, 2, 4):
-                nc.scalar.activation(h[0][:, first : first + count], bank[:, :count], RELU)
+        for first, count, on_vector in ((0, 256, True), (256, 256, False), (512, 256, False), (768, 128, True), (896, 128, False)):
+            piece = psum_h.tile([P, BANK], F32, name="acc_h")
+            multiply_w1(piece[:, :count], 0, first, count)
+            if on_vector:
+                nc.vector.tensor_scalar_max(h[0][:, first : first + count], piece[:, :count], 0.0)
             else:
-                nc.vector.tensor_scalar_max(h[0][:, first : first + count], bank[:, :count], 0.0)
-            first = first + count
+                nc.scalar.activation(h[0][:, first : first + count], piece[:, :count], RELU)
         for t in range(1, PACK):
             low = psum_h.tile([P, BANK], F32, name="acc_h")
             multiply_w1(low[:], t, 0, BANK)
             nc.scalar.activation(h[t][:, :BANK], low[:], RELU)
             high = psum_h.tile([P, BANK], F32, name="acc_h")
-            multiply_w1(high[:, :LAST], t, BANK, LAST)
-            multiply_w1(high[:, LAST:], t, S - LAST, LAST)
+            multiply_w1(high[:, : early_words - BANK], t, BANK, early_words - BANK)
+            multiply_w1(high[:, early_words - BANK :], t, early_words, LATE_WORDS)
             nc.scalar.activation(h[t][:, BANK:], high[:], RELU)
 
-        z_planes = keep.tile([P, PACK, V], BF16, name="z_planes", align_bytes=64)
-        c_planes = keep.tile([P, PACK, V], BF16, name="c_planes", align_bytes=64)
-        z_in = keep.tile([P, V, PACK], BF16, name="z_in", align_bytes=64)
+        z_slabs = keep.tile([P, PACK, V], BF16, name="z_slabs", align_bytes=64)
+        c_slabs = keep.tile([P, PACK, V], BF16, name="c_slabs", align_bytes=64)
+        z_woven = keep.tile([P, V, PACK], BF16, name="z_woven", align_bytes=64)
 
-        def gather_near(dst, t, v0, v1):
-            for d in range(4):
+        def gather_neighbours(dst, t, v0, v1):
+            for d in range(NEIGHBOURS):
                 nc.vector.tensor_copy(dst[:, d, :], h[t][:].indirect(entries(pos_sb[d], v0, v1)))
 
-        def weave(dst, planes, t0, t1, v0, v1):
-            nc.scalar.copy(
-                dst[:, v0:v1, t0:t1].rearrange("p (c i) t -> p c t i", i=4), planes[:, t0:t1, v0:v1].rearrange("p t (c i) -> p c t i", i=4)
-            )
+        def weave(dst, slabs):
+            nc.scalar.copy(dst.rearrange("p (c i) t -> p c t i", i=4), slabs.rearrange("p t (c i) -> p c t i", i=4))
 
-        def quantize(values, v0, v1, name):
-            codes = keep.tile([P, v1 - v0], U32, name=name + "_codes", align_bytes=64)
-            plane = keep.tile([P, v1 - v0], U8, name=name + "_plane", align_bytes=64)
-            nc.vector.quantize_mx(out=codes[:].bitcast(FP8X4), scales=plane[:], in_=values[:, v0:v1, :].rearrange("p v t -> p (v t)"))
+        def quantize(woven, name):
+            count = woven.shape[1]
+            codes = keep.tile([P, count], U32, name=name + "_codes", align_bytes=64)
+            plane = keep.tile([P, count], U8, name=name + "_plane", align_bytes=64)
+            nc.vector.quantize_mx(out=codes[:].bitcast(FP8X4), scales=plane[:], in_=woven.rearrange("p v t -> p (v t)"))
             return codes, plane
 
-        near = [keep.tile([P, 4, V], BF16, name="near%d" % t) for t in range(3)]
-        near3_early = keep.tile([P, 4, EARLY], BF16, name="near3_early")
-        gather_near(near[0], 0, 0, V)
-        gather_near(near[1], 1, 0, V)
+        near = [keep.tile([P, NEIGHBOURS, V], BF16, name="near%d" % t) for t in range(PACK - 1)]
+        near3_early = keep.tile([P, NEIGHBOURS, EARLY], BF16, name="near3_early")
+        gather_neighbours(near[0], 0, 0, V)
+        gather_neighbours(near[1], 1, 0, V)
         for t in range(PACK):
-            nc.vector.tensor_copy(c_planes[:, t, :], h[t][:].indirect(cen_sb[:]))
-        gather_near(near[2], 2, 0, V)
-        gather_near(near3_early, 3, 0, EARLY)
+            nc.vector.tensor_copy(c_slabs[:, t, :], h[t][:].indirect(cen_sb[:]))
+        gather_neighbours(near[2], 2, 0, V)
+        gather_neighbours(near3_early, 3, 0, EARLY)
 
-        def excess(a, b, diff, over):
+        def row(name, tag):
+            return keep.tile([P, V], F32, name=name, tag=tag, align_bytes=64)
+
+        def excess(over, diff, a, b):
             nc.gpsimd.tensor_tensor(diff[:], a, b, SUB)
-            nc.scalar.activation(over[:], diff[:], RELU)
+            nc.scalar.activation(over, diff[:], RELU)
 
-        def shared_row(name, offset):
-            return shared.tile([P, V], F32, name=name, offset=offset, align_bytes=64)
+        pairs0 = keep.tile([P, 2, V], BF16, name="pairs0")
+        pairs1 = keep.tile([P, 2, V], BF16, name="pairs1")
+        pair2_a = keep.tile([P, V], BF16, name="pair2_a")
+        over0_a, over0_b = row("over0_a", "over0_a_then_diff1_a"), row("over0_b", "over0_b_then_diff1_b")
+        excess(over0_a[:], row("diff0_a", "diff0_a"), near[0][:, 0, :], near[0][:, 1, :])
+        excess(over0_b[:], row("diff0_b", "diff0_b"), near[0][:, 2, :], near[0][:, 3, :])
+        nc.gpsimd.tensor_tensor(pairs0[:, 0, :], near[0][:, 1, :], over0_a[:], ADD)
+        nc.gpsimd.tensor_tensor(pairs0[:, 1, :], near[0][:, 3, :], over0_b[:], ADD)
+        over1 = keep.tile([P, 2, V], F32, name="over1", tag="over1_then_diff2_then_centres", align_bytes=64)
+        over0_both = row("over0_both", "over0_both")
+        excess(over1[:, 0, :], row("diff1_a", "over0_a_then_diff1_a"), near[1][:, 0, :], near[1][:, 1, :])
+        excess(over0_both[:], row("diff0_both", "diff0_both"), pairs0[:, 0, :], pairs0[:, 1, :])
+        excess(over1[:, 1, :], row("diff1_b", "over0_b_then_diff1_b"), near[1][:, 2, :], near[1][:, 3, :])
+        nc.gpsimd.tensor_tensor(z_slabs[:, 0, :], pairs0[:, 1, :], over0_both[:], ADD)
+        nc.gpsimd.tensor_tensor(pairs1[:], near[1][:, 1:NEIGHBOURS:2, :], over1[:], ADD)
+        pair3_bytes, pair2_bytes, over_bytes = 2 * EARLY * 2, V * 2, V * 4
+        over1_both = row("over1_both", "over1_both")
+        over2_a = after_gpsimd.tile([P, V], F32, name="over2_a", offset=pair3_bytes - over_bytes // 8, align_bytes=64)
+        excess(over1_both[:], row("diff1_both", "diff1_both_then_centres"), pairs1[:, 0, :], pairs1[:, 1, :])
+        excess(over2_a[:], row("diff2_a", "over1_then_diff2_then_centres"), near[2][:, 0, :], near[2][:, 1, :])
+        nc.gpsimd.tensor_tensor(z_slabs[:, 1, :], pairs1[:, 1, :], over1_both[:], ADD)
+        nc.gpsimd.tensor_tensor(pair2_a[:], near[2][:, 1, :], over2_a[:], ADD)
 
-        diffs = [keep.tile([P, V], F32, name="diff%d" % n) for n in range(3)]
-        diffs = diffs + [shared_row("diff3", 0), shared_row("diff4", 2048), shared_row("diff5", 6144), shared_row("diff6", 12288)]
-        both_overs = shared.tile([P, 2, V], F32, name="both_overs", offset=12288, align_bytes=64)
-        overs = [shared_row("over0", 0), shared_row("over1", 2048), keep.tile([P, V], F32, name="over2"), both_overs[:, 0, :], both_overs[:, 1, :]]
-        overs = overs + [keep.tile([P, V], F32, name="over5"), shared_row("over6", 9472)]
-        pairs = [keep.tile([P, 2, V], BF16, name="pair%d" % t) for t in range(2)] + [keep.tile([P, 1, V], BF16, name="pair2")]
-
-        def start_pair(t, d):
-            excess(near[t][:, 2 * d, :], near[t][:, 2 * d + 1, :], diffs[3 * t + d], overs[3 * t + d])
-
-        def finish_pair(t, d):
-            nc.gpsimd.tensor_tensor(pairs[t][:, d, :], near[t][:, 2 * d + 1, :], overs[3 * t + d][:], ADD)
-
-        def start_slab(t):
-            excess(pairs[t][:, 0, :], pairs[t][:, 1, :], diffs[3 * t + 2], overs[3 * t + 2])
-
-        def finish_slab(t):
-            nc.gpsimd.tensor_tensor(z_planes[:, t, :], pairs[t][:, 1, :], overs[3 * t + 2][:], ADD)
-
-        start_pair(0, 0)
-        start_pair(0, 1)
-        finish_pair(0, 0)
-        finish_pair(0, 1)
-        start_pair(1, 0)
-        start_slab(0)
-        start_pair(1, 1)
-        finish_slab(0)
-        nc.gpsimd.tensor_tensor(pairs[1][:], near[1][:, 1:4:2, :], both_overs[:], ADD)
-        start_slab(1)
-        start_pair(2, 0)
-        finish_slab(1)
-        finish_pair(2, 0)
-
-        c_in = [shared.tile([P, HALF, PACK], BF16, name="c_in%d" % n, offset=offset, align_bytes=64) for n, offset in enumerate((6144, 12288))]
+        c_woven = [
+            keep.tile([P, HALF, PACK], BF16, name="c_woven%d" % n, tag=tag, align_bytes=64)
+            for n, tag in enumerate(("diff1_both_then_centres", "over1_then_diff2_then_centres"))
+        ]
         for n in range(2):
-            weave(c_in[n], c_planes[:, :, n * HALF : (n + 1) * HALF], 0, PACK, 0, HALF)
-        weave(z_in, z_planes, 0, 2, 0, V)
-        pair3_early = shared.tile([P, 2, EARLY], BF16, name="pair3_early", offset=8192, align_bytes=64)
-        pair2_second = shared.tile([P, V], BF16, name="pair2_second", offset=9728, align_bytes=64)
-        near3_late = shared.tile([P, 4, V - EARLY], BF16, name="near3_late", offset=10752, align_bytes=64)
-        pair3_late = keep.tile([P, 2, V - EARLY], BF16, name="pair3_late")
-        nc.vector.tensor_tensor(pair2_second[:], near[2][:, 2, :], near[2][:, 3, :], MAX)
-        nc.vector.tensor_tensor(pair3_early[:], near3_early[:, 0:2, :], near3_early[:, 2:4, :], MAX)
-        nc.vector.tensor_tensor(z_planes[:, 2, :], pairs[2][:, 0, :], pair2_second[:], MAX)
-        nc.vector.tensor_tensor(z_planes[:, 3, :EARLY], pair3_early[:, 0, :], pair3_early[:, 1, :], MAX)
+            weave(c_woven[n][:], c_slabs[:, :, n * HALF : (n + 1) * HALF])
+        weave(z_woven[:, :, 0:2], z_slabs[:, 0:2, :])
+
+        pairs3_early = after_gpsimd.tile([P, 2, EARLY], BF16, name="pairs3_early", offset=0, align_bytes=64)
+        pair2_b = after_gpsimd.tile([P, V], BF16, name="pair2_b", offset=pair3_bytes, align_bytes=64)
+        near3_late = after_gpsimd.tile([P, NEIGHBOURS, V - EARLY], BF16, name="near3_late", offset=pair3_bytes + pair2_bytes, align_bytes=64)
+        pairs3_late = keep.tile([P, 2, V - EARLY], BF16, name="pairs3_late")
+        nc.vector.tensor_tensor(pair2_b[:], near[2][:, 2, :], near[2][:, 3, :], MAX)
+        nc.vector.tensor_tensor(pairs3_early[:], near3_early[:, 0:2, :], near3_early[:, 2:4, :], MAX)
+        nc.vector.tensor_tensor(z_slabs[:, 2, :], pair2_a[:], pair2_b[:], MAX)
+        nc.vector.tensor_tensor(z_slabs[:, 3, :EARLY], pairs3_early[:, 0, :], pairs3_early[:, 1, :], MAX)
         chunks = ((0, HALF), (HALF, EARLY), (EARLY, V))
         for v0, v1 in chunks[:2]:
-            weave(z_in, z_planes, 2, PACK, v0, v1)
-        gather_near(near3_late, 3, EARLY, V)
-        c_quantized = [quantize(c_in[0], 0, HALF, "c0")]
-        nc.vector.tensor_tensor(pair3_late[:], near3_late[:, 0:2, :], near3_late[:, 2:4, :], MAX)
-        c_quantized.append(quantize(c_in[1], 0, HALF, "c1"))
-        nc.vector.tensor_tensor(z_planes[:, 3, EARLY:], pair3_late[:, 0, :], pair3_late[:, 1, :], MAX)
-        weave(z_in, z_planes, 2, PACK, EARLY, V)
+            weave(z_woven[:, v0:v1, 2:4], z_slabs[:, 2:4, v0:v1])
+        gather_neighbours(near3_late, 3, EARLY, V)
+        c_quantized = [quantize(c_woven[0][:], "c0")]
+        nc.vector.tensor_tensor(pairs3_late[:], near3_late[:, 0:2, :], near3_late[:, 2:4, :], MAX)
+        c_quantized.append(quantize(c_woven[1][:], "c1"))
+        nc.vector.tensor_tensor(z_slabs[:, 3, EARLY:], pairs3_late[:, 0, :], pairs3_late[:, 1, :], MAX)
+        weave(z_woven[:, EARLY:, 2:4], z_slabs[:, 2:4, EARLY:])
+
         acc_out = []
         for v0, v1 in chunks:
             codes, plane = c_quantized[v0 // HALF]
@@ -238,7 +234,7 @@ def tile_picked_sagecat_maxrelu_p_kernel(
             )
             acc_out.append(acc)
         for acc, (v0, v1) in zip(acc_out, chunks):
-            codes, plane = quantize(z_in, v0, v1, "z%d" % v0)
+            codes, plane = quantize(z_woven[:, v0:v1, :], "z%d" % v0)
             nc.tensor.matmul_mx(
                 out=acc[:], lhsT=w3_codes[:].bitcast(FP8X4), lhsT_scale=w3_plane[:],
                 rhs=codes[:].bitcast(FP8X4), rhs_scale=plane[:], start=False, stop=True,

@@ -30,8 +30,8 @@ EARLY = V - 128
 
 
 def load_scale_rows(nc, plane, scales):
-    for r in range(PACK):
-        nc.sync.dma_start(out=plane[r:P:QUADRANT, :].bitcast(I32), in_=scales[0, r : PACK * PACK : PACK, :].bitcast(I32))
+    for q in range(P // QUADRANT):
+        nc.sync.dma_start(out=plane[QUADRANT * q : QUADRANT * q + 4, :].bitcast(I32), in_=scales[0, 4 * q : 4 * q + 4, :].bitcast(I32))
 
 
 def words_of(dram_words):
@@ -63,10 +63,9 @@ def tile_picked_sagecat_maxrelu_p_kernel(
         w1_early = keep.tile([P, 2, H], F32, name="w1_early")
         w1_late = keep.tile([P, 2, H], F32, name="w1_late")
         xw_all = keep.tile([P, T], I32, name="xw_all", align_bytes=64)
-        nc.sync.dma_start(out=w1_early[:, 0, :], in_=w1_rows[:, 0, :])
+        nc.sync.dma_start(out=w1_early[:], in_=w1_rows[:, 0:2, :])
         nc.sync.dma_start(offs_sb[:], offs)
         load_scale_rows(nc, xs_all, x_scales)
-        nc.sync.dma_start(out=w1_early[:, 1, :], in_=w1_rows[:, 1, :])
         nc.sync.dma_start(out=xw_all[:], in_=words_of(x_words))
         nc.sync.dma_start(out=w1_late[:], in_=w1_rows[:, 2:4, :])
         for offsets, pos in zip(pos_sb, (pos1, pos2, pos3, pos4)):
@@ -94,8 +93,7 @@ def tile_picked_sagecat_maxrelu_p_kernel(
         w1_others = keep.tile([P, PACK - 1, P, PACK], BF16, name="w1_others", align_bytes=64)
         early_rows, late_rows = [raw[:].rearrange("p j (m t) -> p m t j", t=PACK) for raw in (w1_early, w1_late)]
         others_by_place = w1_others[:].rearrange("p t m j -> p m t j")
-        for j in range(2):
-            nc.scalar.copy(w1_slab0[:, :, j], early_rows[:, :, 0, j])
+        nc.scalar.copy(w1_slab0[:, :, 0:2], early_rows[:, :, 0, :])
         nc.scalar.copy(others_by_place[:, :, :, 0:2], early_rows[:, :, 1:PACK, :])
         nc.scalar.copy(w1_slab0[:, : P // 2, 2:4], late_rows[:, : P // 2, 0, :])
         nc.gpsimd.tensor_scalar(w1_slab0[:, P // 2 :, 2:4], late_rows[:, P // 2 :, 0, :], 1.0, 0.0, MULT, ADD)

@@ -50,6 +50,7 @@ def tile_picked_sagecat_maxrelu_p_kernel(
         lists = ctx.enter_context(tc.tile_pool(name="lists", bufs=1))
         keep = ctx.enter_context(tc.tile_pool(name="keep", bufs=1))
         after_gpsimd = ctx.enter_context(tc.tile_pool(name="after_gpsimd", bufs=1))
+        centres = ctx.enter_context(tc.tile_pool(name="centres", bufs=1))
         psum_h = ctx.enter_context(tc.psum_pool(name="psum_h", bufs=5))
         psum_out = ctx.enter_context(tc.psum_pool(name="psum_out", bufs=3))
 
@@ -149,24 +150,25 @@ def tile_picked_sagecat_maxrelu_p_kernel(
         def weave(dst, slabs):
             nc.scalar.copy(dst.rearrange("p (c i) t -> p c t i", i=4), slabs.rearrange("p t (c i) -> p c t i", i=4))
 
-        def quantize(woven, name):
+        def quantize(woven, name, plane=None):
             count = woven.shape[1]
             codes = keep.tile([P, count], U32, name=name + "_codes", align_bytes=64)
-            plane = keep.tile([P, count], U8, name=name + "_plane", align_bytes=64)
+            if plane is None:
+                plane = keep.tile([P, count], U8, name=name + "_plane", align_bytes=64)
             nc.vector.quantize_mx(out=codes[:].bitcast(FP8X4), scales=plane[:], in_=woven.rearrange("p v t -> p (v t)"))
             return codes, plane
 
-        near = [keep.tile([P, NEIGHBOURS, V], BF16, name="near%d" % t) for t in range(PACK - 1)]
-        near3_early = keep.tile([P, NEIGHBOURS, EARLY], BF16, name="near3_early")
+        near = [keep.tile([P, NEIGHBOURS, V], BF16, name="near%d" % t) for t in range(2)]
         gather_neighbours(near[0], 0, 0, V)
         gather_neighbours(near[1], 1, 0, V)
         for t in range(PACK):
             nc.vector.tensor_copy(c_slabs[:, t, :], h[t][:].indirect(cen_sb[:]))
-        gather_neighbours(near[2], 2, 0, V)
-        gather_neighbours(near3_early, 3, 0, EARLY)
 
         def row(name, tag):
             return keep.tile([P, V], F32, name=name, tag=tag, align_bytes=64)
+
+        def row_under_centres(name, n):
+            return centres.tile([P, V], F32, name=name, offset=n * V * 4, align_bytes=64)
 
         def excess(over, diff, a, b):
             nc.gpsimd.tensor_tensor(diff[:], a, b, SUB)
@@ -175,30 +177,32 @@ def tile_picked_sagecat_maxrelu_p_kernel(
         pairs0 = keep.tile([P, 2, V], BF16, name="pairs0")
         pairs1 = keep.tile([P, 2, V], BF16, name="pairs1")
         pair2_a = keep.tile([P, V], BF16, name="pair2_a")
-        over0_a, over0_b = row("over0_a", "over0_a_then_diff1_a"), row("over0_b", "over0_b_then_diff1_b")
-        excess(over0_a[:], row("diff0_a", "diff0_a"), near[0][:, 0, :], near[0][:, 1, :])
-        excess(over0_b[:], row("diff0_b", "diff0_b"), near[0][:, 2, :], near[0][:, 3, :])
+        over0_a, over0_b = row("over0_a", "over0_a_then_diff1_a"), row_under_centres("over0_b", 1)
+        excess(over0_a[:], row("diff0_a", "diff0_a_then_near2"), near[0][:, 0, :], near[0][:, 1, :])
+        excess(over0_b[:], row("diff0_b", "diff0_b_then_near3"), near[0][:, 2, :], near[0][:, 3, :])
+        near.append(keep.tile([P, NEIGHBOURS, V], BF16, name="near2", tag="diff0_a_then_near2", align_bytes=64))
+        near3_early = keep.tile([P, NEIGHBOURS, EARLY], BF16, name="near3_early", tag="diff0_b_then_near3", align_bytes=64)
+        gather_neighbours(near[2], 2, 0, V)
+        gather_neighbours(near3_early, 3, 0, EARLY)
         nc.gpsimd.tensor_tensor(pairs0[:, 0, :], near[0][:, 1, :], over0_a[:], ADD)
         nc.gpsimd.tensor_tensor(pairs0[:, 1, :], near[0][:, 3, :], over0_b[:], ADD)
         over1 = keep.tile([P, 2, V], F32, name="over1", tag="over1_then_diff2_then_centres", align_bytes=64)
         over0_both = row("over0_both", "over0_both")
         excess(over1[:, 0, :], row("diff1_a", "over0_a_then_diff1_a"), near[1][:, 0, :], near[1][:, 1, :])
-        excess(over0_both[:], row("diff0_both", "diff0_both"), pairs0[:, 0, :], pairs0[:, 1, :])
-        excess(over1[:, 1, :], row("diff1_b", "over0_b_then_diff1_b"), near[1][:, 2, :], near[1][:, 3, :])
+        excess(over0_both[:], row_under_centres("diff0_both", 0), pairs0[:, 0, :], pairs0[:, 1, :])
+        excess(over1[:, 1, :], row_under_centres("diff1_b", 1), near[1][:, 2, :], near[1][:, 3, :])
         nc.gpsimd.tensor_tensor(z_slabs[:, 0, :], pairs0[:, 1, :], over0_both[:], ADD)
         nc.gpsimd.tensor_tensor(pairs1[:], near[1][:, 1:NEIGHBOURS:2, :], over1[:], ADD)
         pair3_bytes, pair2_bytes, over_bytes = 2 * EARLY * 2, V * 2, V * 4
         over1_both = row("over1_both", "over1_both")
-        over2_a = after_gpsimd.tile([P, V], F32, name="over2_a", offset=pair3_bytes - over_bytes // 8, align_bytes=64)
+        over2_a = after_gpsimd.tile([P, 2, V], F32, name="over2_a", offset=pair3_bytes - over_bytes // 8, align_bytes=64)[:, 0, :]
         excess(over1_both[:], row("diff1_both", "diff1_both_then_centres"), pairs1[:, 0, :], pairs1[:, 1, :])
         excess(over2_a[:], row("diff2_a", "over1_then_diff2_then_centres"), near[2][:, 0, :], near[2][:, 1, :])
         nc.gpsimd.tensor_tensor(z_slabs[:, 1, :], pairs1[:, 1, :], over1_both[:], ADD)
         nc.gpsimd.tensor_tensor(pair2_a[:], near[2][:, 1, :], over2_a[:], ADD)
 
-        c_woven = [
-            keep.tile([P, HALF, PACK], BF16, name="c_woven%d" % n, tag=tag, align_bytes=64)
-            for n, tag in enumerate(("diff1_both_then_centres", "over1_then_diff2_then_centres"))
-        ]
+        c_all = centres.tile([P, V, PACK], BF16, name="c_woven", offset=0, align_bytes=64)
+        c_woven = [c_all[:, n * HALF : (n + 1) * HALF, :] for n in range(2)]
         for n in range(2):
             weave(c_woven[n][:], c_slabs[:, :, n * HALF : (n + 1) * HALF])
         weave(z_woven[:, :, 0:2], z_slabs[:, 0:2, :])
@@ -215,9 +219,11 @@ def tile_picked_sagecat_maxrelu_p_kernel(
         for v0, v1 in chunks[:2]:
             weave(z_woven[:, v0:v1, 2:4], z_slabs[:, 2:4, v0:v1])
         gather_neighbours(near3_late, 3, EARLY, V)
-        c_quantized = [quantize(c_woven[0][:], "c0")]
+        planes_at = pair3_bytes + pair2_bytes + NEIGHBOURS * (V - EARLY) * 2
+        c_planes = [after_gpsimd.tile([P, HALF], U8, name="c_plane%d" % n, offset=planes_at + n * HALF, align_bytes=64) for n in range(2)]
+        c_quantized = [quantize(c_woven[0][:], "c0", c_planes[0])]
         nc.vector.tensor_tensor(pairs3_late[:], near3_late[:, 0:2, :], near3_late[:, 2:4, :], MAX)
-        c_quantized.append(quantize(c_woven[1][:], "c1"))
+        c_quantized.append(quantize(c_woven[1][:], "c1", c_planes[1]))
         nc.vector.tensor_tensor(z_slabs[:, 3, EARLY:], pairs3_late[:, 0, :], pairs3_late[:, 1, :], MAX)
         weave(z_woven[:, EARLY:, 2:4], z_slabs[:, 2:4, EARLY:])
 

@@ -13,10 +13,10 @@ U16 = mybir.dt.uint16
 U8 = mybir.dt.uint8
 FP8X4 = mybir.dt.float8_e4m3fn_x4
 RELU = mybir.ActivationFunctionType.Relu
+COPY = mybir.ActivationFunctionType.Copy
 MAX = mybir.AluOpType.max
 MULT = mybir.AluOpType.mult
 ADD = mybir.AluOpType.add
-SUB = mybir.AluOpType.subtract
 
 P = 128
 PACK = 4
@@ -24,9 +24,8 @@ QUADRANT = 32
 BANK = 512
 LIST_ROWS = 16
 NEIGHBOURS = 4
-LATE_WORDS = 256
 HALF = V // 2
-EARLY = V - 128
+QUARTER = V // 4
 
 
 def load_scale_rows(nc, plane, scales):
@@ -49,8 +48,6 @@ def tile_picked_sagecat_maxrelu_p_kernel(
     with ExitStack() as ctx:
         lists = ctx.enter_context(tc.tile_pool(name="lists", bufs=1))
         keep = ctx.enter_context(tc.tile_pool(name="keep", bufs=1))
-        after_gpsimd = ctx.enter_context(tc.tile_pool(name="after_gpsimd", bufs=1))
-        centres = ctx.enter_context(tc.tile_pool(name="centres", bufs=1))
         psum_h = ctx.enter_context(tc.psum_pool(name="psum_h", bufs=5))
         psum_out = ctx.enter_context(tc.psum_pool(name="psum_out", bufs=3))
 
@@ -67,8 +64,8 @@ def tile_picked_sagecat_maxrelu_p_kernel(
         nc.sync.dma_start(out=w1_early[:], in_=w1_rows[:, 0:2, :])
         nc.sync.dma_start(offs_sb[:], offs)
         load_scale_rows(nc, xs_all, x_scales)
-        nc.sync.dma_start(out=xw_all[:], in_=words_of(x_words))
         nc.sync.dma_start(out=w1_late[:], in_=w1_rows[:, 2:4, :])
+        nc.sync.dma_start(out=xw_all[:], in_=words_of(x_words))
         for offsets, pos in zip(pos_sb, (pos1, pos2, pos3, pos4)):
             nc.sync.dma_start(offsets[:], pos)
         nc.sync.dma_start(cen_sb[:], cen)
@@ -84,161 +81,126 @@ def tile_picked_sagecat_maxrelu_p_kernel(
 
         xs_pick = keep.tile([P, S], U8, name="xs_pick", align_bytes=64)
         nc.vector.tensor_copy(xs_pick[:], xs_all[:].indirect(offs_sb[:]))
-        xw_window = xw_all[:].bitcast(U32)
-        early_words = S - LATE_WORDS
-        xw_early = keep.tile([P, early_words], U32, name="xw_early", align_bytes=64)
-        for first, last in ((0, BANK), (BANK, early_words)):
-            nc.vector.tensor_copy(xw_early[:, first:last], xw_window.indirect(entries(offs_sb, first, last)))
 
-        w1_slab0 = keep.tile([P, P, PACK], BF16, name="w1_slab0", tag="w1_slab0_then_late_words", align_bytes=64)
-        w1_others = keep.tile([P, PACK - 1, P, PACK], BF16, name="w1_others", align_bytes=64)
+        w1_pair = [keep.tile([P, 2, P, PACK], BF16, name="w1_pair%d" % n, align_bytes=64) for n in range(2)]
         early_rows, late_rows = [raw[:].rearrange("p j (m t) -> p m t j", t=PACK) for raw in (w1_early, w1_late)]
-        others_by_place = w1_others[:].rearrange("p t m j -> p m t j")
-        nc.scalar.copy(w1_slab0[:, :, 0:2], early_rows[:, :, 0, :])
-        nc.scalar.copy(others_by_place[:, :, :, 0:2], early_rows[:, :, 1:PACK, :])
-        nc.scalar.copy(w1_slab0[:, : P // 2, 2:4], late_rows[:, : P // 2, 0, :])
-        nc.gpsimd.tensor_scalar(w1_slab0[:, P // 2 :, 2:4], late_rows[:, P // 2 :, 0, :], 1.0, 0.0, MULT, ADD)
-        nc.scalar.copy(others_by_place[:, :, :, 2:4], late_rows[:, :, 1:PACK, :])
-        w1_codes = keep.tile([P, H], U32, name="w1_codes", align_bytes=64)
-        w1_plane = keep.tile([P, H], U8, name="w1_plane", align_bytes=64)
-
-        def quantize_w1(t0, t1, values):
-            cols = slice(t0 * P, t1 * P)
-            nc.vector.quantize_mx(out=w1_codes[:, cols].bitcast(FP8X4), scales=w1_plane[:, cols], in_=values)
-
-        quantize_w1(0, 1, w1_slab0[:].rearrange("p m j -> p (m j)"))
-        xw_late = keep.tile([P, LATE_WORDS], U32, name="xw_late", tag="w1_slab0_then_late_words", align_bytes=64)
-        nc.vector.tensor_copy(xw_late[:], xw_window.indirect(entries(offs_sb, early_words, S)))
-        quantize_w1(1, 2, w1_others[:, 0:1].rearrange("p t m j -> p (t m j)"))
-        quantize_w1(2, 4, w1_others[:, 1:3].rearrange("p t m j -> p (t m j)"))
-
-        def multiply_w1(acc, t, first, count):
-            if first < early_words:
-                words = xw_early[:, first : first + count]
-            else:
-                words = xw_late[:, first - early_words : first - early_words + count]
-            nc.tensor.matmul_mx(
-                out=acc, lhsT=w1_codes[:, t * P : (t + 1) * P].bitcast(FP8X4), lhsT_scale=w1_plane[:, t * P : (t + 1) * P],
-                rhs=words.bitcast(FP8X4), rhs_scale=xs_pick[:, first : first + count], start=True, stop=True,
+        by_place = [pair[:].rearrange("p t m j -> p m t j") for pair in w1_pair]
+        for n in range(2):
+            nc.scalar.copy(by_place[n][:, :, :, 0:2], early_rows[:, :, 2 * n : 2 * n + 2, :])
+        nc.scalar.copy(by_place[0][:, :, :, 2:4], late_rows[:, :, 0:2, :])
+        nc.gpsimd.tensor_scalar(by_place[1][:, :, :, 2:4], late_rows[:, :, 2:4, :], 1.0, 0.0, MULT, ADD)
+        w1_codes = keep.tile([P, H], U32, name="w1_codes", tag="w1_codes_then_centres", align_bytes=64)
+        w1_plane = keep.tile([P, H], U8, name="w1_plane", tag="w1_plane_then_centres", align_bytes=64)
+        for n in range(2):
+            cols = slice(2 * n * P, (2 * n + 2) * P)
+            nc.vector.quantize_mx(
+                out=w1_codes[:, cols].bitcast(FP8X4), scales=w1_plane[:, cols], in_=w1_pair[n][:].rearrange("p t m j -> p (t m j)")
             )
 
+        xw_window = xw_all[:].bitcast(U32)
+        xw_pick = keep.tile([P, S], U32, name="xw_pick", align_bytes=64)
+        for first, last in ((0, 256), (256, 512), (512, 768), (768, 896), (896, S)):
+            nc.vector.tensor_copy(xw_pick[:, first:last], xw_window.indirect(entries(offs_sb, first, last)))
+
         h = [keep.tile([P, S], F32, name="h%d" % t, align_bytes=64) for t in range(PACK)]
-        for first, count, on_vector in ((0, 256, True), (256, 256, False), (512, 256, False), (768, 128, True), (896, 128, False)):
-            piece = psum_h.tile([P, BANK], F32, name="acc_h")
-            multiply_w1(piece[:, :count], 0, first, count)
+
+        def make_h(t, first, last, on_vector=False):
+            acc = psum_h.tile([P, BANK], F32, name="acc_h")[:, : last - first]
+            nc.tensor.matmul_mx(
+                out=acc, lhsT=w1_codes[:, t * P : (t + 1) * P].bitcast(FP8X4), lhsT_scale=w1_plane[:, t * P : (t + 1) * P],
+                rhs=xw_pick[:, first:last].bitcast(FP8X4), rhs_scale=xs_pick[:, first:last], start=True, stop=True,
+            )
             if on_vector:
-                nc.vector.tensor_scalar_max(h[0][:, first : first + count], piece[:, :count], 0.0)
+                nc.vector.tensor_scalar_max(h[t][:, first:last], acc, 0.0)
             else:
-                nc.scalar.activation(h[0][:, first : first + count], piece[:, :count], RELU)
-        for t in range(1, PACK):
-            low = psum_h.tile([P, BANK], F32, name="acc_h")
-            multiply_w1(low[:], t, 0, BANK)
-            nc.scalar.activation(h[t][:, :BANK], low[:], RELU)
-            high = psum_h.tile([P, BANK], F32, name="acc_h")
-            multiply_w1(high[:, : early_words - BANK], t, BANK, early_words - BANK)
-            multiply_w1(high[:, early_words - BANK :], t, early_words, LATE_WORDS)
-            nc.scalar.activation(h[t][:, BANK:], high[:], RELU)
+                nc.scalar.activation(h[t][:, first:last], acc, RELU)
 
-        z_slabs = keep.tile([P, PACK, V], BF16, name="z_slabs", align_bytes=64)
-        c_slabs = keep.tile([P, PACK, V], BF16, name="c_slabs", align_bytes=64)
-        z_woven = keep.tile([P, V, PACK], BF16, name="z_woven", align_bytes=64)
+        def gather(dst, t, offsets, v0, v1, on_vector):
+            window = h[t][:].indirect(entries(offsets, v0, v1))
+            if on_vector:
+                nc.vector.tensor_copy(dst, window)
+            else:
+                nc.scalar.activation(dst, window, COPY)
 
-        def gather_neighbours(dst, t, v0, v1):
-            for d in range(NEIGHBOURS):
-                nc.vector.tensor_copy(dst[:, d, :], h[t][:].indirect(entries(pos_sb[d], v0, v1)))
+        def weave_views(dst, slabs):
+            return dst.rearrange("p (c i) t -> p c t i", i=4), slabs.rearrange("p t (c i) -> p c t i", i=4)
 
-        def weave(dst, slabs):
-            nc.scalar.copy(dst.rearrange("p (c i) t -> p c t i", i=4), slabs.rearrange("p t (c i) -> p c t i", i=4))
+        def weave_on_gpsimd(dst, slabs):
+            nc.gpsimd.tensor_scalar(dst, slabs.rearrange("p t v -> p v t"), 1.0, 0.0, MULT, ADD)
 
-        def quantize(woven, name, plane=None):
+        def quantize(woven, name):
             count = woven.shape[1]
             codes = keep.tile([P, count], U32, name=name + "_codes", align_bytes=64)
-            if plane is None:
-                plane = keep.tile([P, count], U8, name=name + "_plane", align_bytes=64)
+            plane = keep.tile([P, count], U8, name=name + "_plane", align_bytes=64)
             nc.vector.quantize_mx(out=codes[:].bitcast(FP8X4), scales=plane[:], in_=woven.rearrange("p v t -> p (v t)"))
             return codes, plane
 
-        near = [keep.tile([P, NEIGHBOURS, V], BF16, name="near%d" % t) for t in range(2)]
-        gather_neighbours(near[0], 0, 0, V)
-        gather_neighbours(near[1], 1, 0, V)
-        for t in range(PACK):
-            nc.vector.tensor_copy(c_slabs[:, t, :], h[t][:].indirect(cen_sb[:]))
+        for first in (0, 256):
+            make_h(0, first, first + 256)
+            make_h(1, first, first + 256)
+        make_h(0, 512, 768)
+        make_h(1, 512, 768, on_vector=True)
+        make_h(0, 768, 896)
+        make_h(0, 896, S)
+        make_h(1, 768, S)
 
-        def row(name, tag):
-            return keep.tile([P, V], F32, name=name, tag=tag, align_bytes=64)
+        near = keep.tile([P, NEIGHBOURS, PACK, HALF], BF16, name="near_first", tag="near", align_bytes=64)
+        for d in range(NEIGHBOURS):
+            gather(near[:, d, 0, :], 0, pos_sb[d], 0, HALF, True)
+        gather(near[:, 2, 1, :], 1, pos_sb[2], 0, HALF, False)
+        make_h(2, 0, BANK)
+        make_h(2, BANK, S)
+        gather(near[:, 3, 1, :], 1, pos_sb[3], 0, HALF, False)
+        make_h(3, 0, BANK)
+        make_h(3, BANK, S)
+        for t in range(1, PACK):
+            for d in range(NEIGHBOURS):
+                if t > 1 or d < 2:
+                    gather(near[:, d, t, :], t, pos_sb[d], 0, HALF, d < 2)
+        pairs = keep.tile([P, 2, PACK, HALF], BF16, name="pairs", align_bytes=64)
+        z_first = keep.tile([P, PACK, HALF], BF16, name="z_first", align_bytes=64)
+        for t in (0, 2):
+            nc.vector.tensor_tensor(pairs[:, :, t : t + 2, :], near[:, 0:2, t : t + 2, :], near[:, 2:4, t : t + 2, :], MAX)
+        for t in (0, 2):
+            nc.vector.tensor_tensor(z_first[:, t : t + 2, :], pairs[:, 0, t : t + 2, :], pairs[:, 1, t : t + 2, :], MAX)
+        z_woven = keep.tile([P, V, PACK], BF16, name="z_woven", align_bytes=64)
+        weave_on_gpsimd(z_woven[:, :HALF, :], z_first[:])
 
-        def row_under_centres(name, n):
-            return centres.tile([P, V], F32, name=name, offset=n * V * 4, align_bytes=64)
+        c_woven = keep.tile([P, V, PACK], BF16, name="c_woven", align_bytes=64)
+        for v0, tag in ((0, "w1_codes_then_centres"), (HALF, "w1_plane_then_centres")):
+            c_slabs = keep.tile([P, PACK, HALF], BF16, name="c_slabs%d" % v0, tag=tag, align_bytes=64)
+            for t in range(PACK):
+                gather(c_slabs[:, t, :], t, cen_sb, v0, v0 + HALF, False)
+            weave_on_gpsimd(c_woven[:, v0 : v0 + HALF, :], c_slabs[:])
 
-        def excess(over, diff, a, b):
-            nc.gpsimd.tensor_tensor(diff[:], a, b, SUB)
-            nc.scalar.activation(over, diff[:], RELU)
+        near = keep.tile([P, NEIGHBOURS, PACK, HALF], BF16, name="near_second", tag="near", align_bytes=64)
+        for d in range(NEIGHBOURS):
+            for t in range(PACK):
+                gather(near[:, d, t, :], t, pos_sb[d], HALF, V, d < 2)
+        two = keep.tile([P, PACK, HALF], BF16, name="two", align_bytes=64)
+        three = keep.tile([P, PACK, HALF], BF16, name="three", align_bytes=64)
+        z_second = keep.tile([P, PACK, HALF], BF16, name="z_second", align_bytes=64)
+        nc.vector.tensor_tensor(two[:], near[:, 0], near[:, 1], MAX)
+        z_codes = [quantize(z_woven[:, :HALF, :], "z0")]
+        nc.vector.tensor_tensor(three[:], two[:], near[:, 2], MAX)
+        c_codes = [quantize(c_woven[:, :HALF, :], "c0")]
+        nc.vector.tensor_tensor(z_second[:, 0:3, :], three[:, 0:3, :], near[:, 3, 0:3, :], MAX)
+        nc.vector.tensor_tensor(z_second[:, 3, :], three[:, 3, :], near[:, 3, 3, :], MAX)
+        c_codes.append(quantize(c_woven[:, HALF:, :], "c1"))
+        nc.vector.tensor_copy(*weave_views(z_woven[:, HALF : HALF + QUARTER, :], z_second[:, :, :QUARTER]))
+        nc.scalar.copy(*weave_views(z_woven[:, HALF + QUARTER :, :], z_second[:, :, QUARTER:]))
+        z_codes.append(quantize(z_woven[:, HALF : HALF + QUARTER, :], "z1"))
+        z_codes.append(quantize(z_woven[:, HALF + QUARTER :, :], "z2"))
 
-        pairs0 = keep.tile([P, 2, V], BF16, name="pairs0")
-        pairs1 = keep.tile([P, 2, V], BF16, name="pairs1")
-        pair2_a = keep.tile([P, V], BF16, name="pair2_a")
-        over0_a, over0_b = row("over0_a", "over0_a_then_diff1_a"), row_under_centres("over0_b", 1)
-        excess(over0_a[:], row("diff0_a", "diff0_a_then_near2"), near[0][:, 0, :], near[0][:, 1, :])
-        excess(over0_b[:], row("diff0_b", "diff0_b_then_near3"), near[0][:, 2, :], near[0][:, 3, :])
-        near.append(keep.tile([P, NEIGHBOURS, V], BF16, name="near2", tag="diff0_a_then_near2", align_bytes=64))
-        near3_early = keep.tile([P, NEIGHBOURS, EARLY], BF16, name="near3_early", tag="diff0_b_then_near3", align_bytes=64)
-        gather_neighbours(near[2], 2, 0, V)
-        gather_neighbours(near3_early, 3, 0, EARLY)
-        nc.gpsimd.tensor_tensor(pairs0[:, 0, :], near[0][:, 1, :], over0_a[:], ADD)
-        nc.gpsimd.tensor_tensor(pairs0[:, 1, :], near[0][:, 3, :], over0_b[:], ADD)
-        over1 = keep.tile([P, 2, V], F32, name="over1", tag="over1_then_diff2_then_centres", align_bytes=64)
-        over0_both = row("over0_both", "over0_both")
-        excess(over1[:, 0, :], row("diff1_a", "over0_a_then_diff1_a"), near[1][:, 0, :], near[1][:, 1, :])
-        excess(over0_both[:], row_under_centres("diff0_both", 0), pairs0[:, 0, :], pairs0[:, 1, :])
-        excess(over1[:, 1, :], row_under_centres("diff1_b", 1), near[1][:, 2, :], near[1][:, 3, :])
-        nc.gpsimd.tensor_tensor(z_slabs[:, 0, :], pairs0[:, 1, :], over0_both[:], ADD)
-        nc.gpsimd.tensor_tensor(pairs1[:], near[1][:, 1:NEIGHBOURS:2, :], over1[:], ADD)
-        pair3_bytes, pair2_bytes, over_bytes = 2 * EARLY * 2, V * 2, V * 4
-        over1_both = row("over1_both", "over1_both")
-        over2_a = after_gpsimd.tile([P, 2, V], F32, name="over2_a", offset=pair3_bytes - over_bytes // 8, align_bytes=64)[:, 0, :]
-        excess(over1_both[:], row("diff1_both", "diff1_both_then_centres"), pairs1[:, 0, :], pairs1[:, 1, :])
-        excess(over2_a[:], row("diff2_a", "over1_then_diff2_then_centres"), near[2][:, 0, :], near[2][:, 1, :])
-        nc.gpsimd.tensor_tensor(z_slabs[:, 1, :], pairs1[:, 1, :], over1_both[:], ADD)
-        nc.gpsimd.tensor_tensor(pair2_a[:], near[2][:, 1, :], over2_a[:], ADD)
-
-        c_all = centres.tile([P, V, PACK], BF16, name="c_woven", offset=0, align_bytes=64)
-        c_woven = [c_all[:, n * HALF : (n + 1) * HALF, :] for n in range(2)]
-        for n in range(2):
-            weave(c_woven[n][:], c_slabs[:, :, n * HALF : (n + 1) * HALF])
-        weave(z_woven[:, :, 0:2], z_slabs[:, 0:2, :])
-
-        pairs3_early = after_gpsimd.tile([P, 2, EARLY], BF16, name="pairs3_early", offset=0, align_bytes=64)
-        pair2_b = after_gpsimd.tile([P, V], BF16, name="pair2_b", offset=pair3_bytes, align_bytes=64)
-        near3_late = after_gpsimd.tile([P, NEIGHBOURS, V - EARLY], BF16, name="near3_late", offset=pair3_bytes + pair2_bytes, align_bytes=64)
-        pairs3_late = keep.tile([P, 2, V - EARLY], BF16, name="pairs3_late")
-        nc.vector.tensor_tensor(pair2_b[:], near[2][:, 2, :], near[2][:, 3, :], MAX)
-        nc.vector.tensor_tensor(pairs3_early[:], near3_early[:, 0:2, :], near3_early[:, 2:4, :], MAX)
-        nc.vector.tensor_tensor(z_slabs[:, 2, :], pair2_a[:], pair2_b[:], MAX)
-        nc.vector.tensor_tensor(z_slabs[:, 3, :EARLY], pairs3_early[:, 0, :], pairs3_early[:, 1, :], MAX)
-        chunks = ((0, HALF), (HALF, EARLY), (EARLY, V))
-        for v0, v1 in chunks[:2]:
-            weave(z_woven[:, v0:v1, 2:4], z_slabs[:, 2:4, v0:v1])
-        gather_neighbours(near3_late, 3, EARLY, V)
-        planes_at = pair3_bytes + pair2_bytes + NEIGHBOURS * (V - EARLY) * 2
-        c_planes = [after_gpsimd.tile([P, HALF], U8, name="c_plane%d" % n, offset=planes_at + n * HALF, align_bytes=64) for n in range(2)]
-        c_quantized = [quantize(c_woven[0][:], "c0", c_planes[0])]
-        nc.vector.tensor_tensor(pairs3_late[:], near3_late[:, 0:2, :], near3_late[:, 2:4, :], MAX)
-        c_quantized.append(quantize(c_woven[1][:], "c1", c_planes[1]))
-        nc.vector.tensor_tensor(z_slabs[:, 3, EARLY:], pairs3_late[:, 0, :], pairs3_late[:, 1, :], MAX)
-        weave(z_woven[:, EARLY:, 2:4], z_slabs[:, 2:4, EARLY:])
-
-        acc_out = []
-        for v0, v1 in chunks:
-            codes, plane = c_quantized[v0 // HALF]
-            cols = slice(v0 % HALF, v0 % HALF + v1 - v0)
+        chunks = ((0, HALF), (HALF, HALF + QUARTER), (HALF + QUARTER, V))
+        for (v0, v1), (codes, plane) in zip(chunks, z_codes):
             acc = psum_out.tile([P, v1 - v0], F32, name="acc_out")
+            centre_codes, centre_plane = c_codes[v0 // HALF]
+            cols = slice(v0 % HALF, v0 % HALF + v1 - v0)
             nc.tensor.matmul_mx(
                 out=acc[:], lhsT=w2_codes[:].bitcast(FP8X4), lhsT_scale=w2_plane[:],
-                rhs=codes[:, cols].bitcast(FP8X4), rhs_scale=plane[:, cols], start=True, stop=False,
+                rhs=centre_codes[:, cols].bitcast(FP8X4), rhs_scale=centre_plane[:, cols], start=True, stop=False,
             )
-            acc_out.append(acc)
-        for acc, (v0, v1) in zip(acc_out, chunks):
-            codes, plane = quantize(z_woven[:, v0:v1, :], "z%d" % v0)
             nc.tensor.matmul_mx(
                 out=acc[:], lhsT=w3_codes[:].bitcast(FP8X4), lhsT_scale=w3_plane[:],
                 rhs=codes[:].bitcast(FP8X4), rhs_scale=plane[:], start=False, stop=True,

@@ -176,7 +176,10 @@ def tile_picked_sagecat_maxrelu_p_kernel(
         near = keep.tile([P, NEIGHBOURS, PACK, HALF], BF16, name="near_second", tag="near", align_bytes=64)
         for d in range(NEIGHBOURS):
             for t in range(PACK):
-                gather(near[:, d, t, :], t, pos_sb[d], HALF, V, d < 2)
+                if (d, t) != (NEIGHBOURS - 1, PACK - 1):
+                    gather(near[:, d, t, :], t, pos_sb[d], HALF, V, d < 2 or (d, t) == (2, 0))
+        for v0 in (0, QUARTER):
+            gather(near[:, 3, 3, v0 : v0 + QUARTER], 3, pos_sb[3], HALF + v0, HALF + v0 + QUARTER, False)
         two = keep.tile([P, PACK, HALF], BF16, name="two", align_bytes=64)
         three = keep.tile([P, PACK, HALF], BF16, name="three", align_bytes=64)
         z_second = keep.tile([P, PACK, HALF], BF16, name="z_second", align_bytes=64)
@@ -185,10 +188,11 @@ def tile_picked_sagecat_maxrelu_p_kernel(
         nc.vector.tensor_tensor(three[:], two[:], near[:, 2], MAX)
         c_codes = [quantize(c_woven[:, :HALF, :], "c0")]
         nc.vector.tensor_tensor(z_second[:, 0:3, :], three[:, 0:3, :], near[:, 3, 0:3, :], MAX)
-        nc.vector.tensor_tensor(z_second[:, 3, :], three[:, 3, :], near[:, 3, 3, :], MAX)
-        c_codes.append(quantize(c_woven[:, HALF:, :], "c1"))
+        nc.vector.tensor_tensor(z_second[:, 3, :QUARTER], three[:, 3, :QUARTER], near[:, 3, 3, :QUARTER], MAX)
+        nc.vector.tensor_tensor(z_second[:, 3, QUARTER:], three[:, 3, QUARTER:], near[:, 3, 3, QUARTER:], MAX)
         nc.vector.tensor_copy(*weave_views(z_woven[:, HALF : HALF + QUARTER, :], z_second[:, :, :QUARTER]))
         nc.scalar.copy(*weave_views(z_woven[:, HALF + QUARTER :, :], z_second[:, :, QUARTER:]))
+        c_codes.append(quantize(c_woven[:, HALF:, :], "c1"))
         z_codes.append(quantize(z_woven[:, HALF : HALF + QUARTER, :], "z1"))
         z_codes.append(quantize(z_woven[:, HALF + QUARTER :, :], "z2"))
 

@@ -26,6 +26,8 @@ LIST_ROWS = 16
 NEIGHBOURS = 4
 HALF = V // 2
 QUARTER = V // 4
+BANKS = 8
+CUTS = (0, 128, 384, 640, 896, S)
 
 
 def load_scale_rows(nc, plane, scales):
@@ -48,8 +50,12 @@ def tile_picked_sagecat_maxrelu_p_kernel(
     with ExitStack() as ctx:
         lists = ctx.enter_context(tc.tile_pool(name="lists", bufs=1))
         keep = ctx.enter_context(tc.tile_pool(name="keep", bufs=1))
-        psum_h = ctx.enter_context(tc.psum_pool(name="psum_h", bufs=5))
-        psum_out = ctx.enter_context(tc.psum_pool(name="psum_out", bufs=3))
+        psum = ctx.enter_context(tc.psum_pool(name="psum", bufs=1))
+        taken = []
+
+        def next_bank(count):
+            taken.append(count)
+            return psum.tile([P, BANK], F32, name="acc", tag="bank%d" % (len(taken) % BANKS))[:, :count]
 
         xs_all = keep.tile([P, T], U8, name="xs_all", align_bytes=64)
         nc.vector.memset(xs_all[:, : T // 2].bitcast(I32), 0)
@@ -99,17 +105,20 @@ def tile_picked_sagecat_maxrelu_p_kernel(
 
         xw_window = xw_all[:].bitcast(U32)
         xw_pick = keep.tile([P, S], U32, name="xw_pick", align_bytes=64)
-        for first, last in ((0, 256), (256, 512), (512, 768), (768, 896), (896, S)):
+        for first, last in zip(CUTS, CUTS[1:]):
             nc.vector.tensor_copy(xw_pick[:, first:last], xw_window.indirect(entries(offs_sb, first, last)))
 
         h = [keep.tile([P, S], F32, name="h%d" % t, align_bytes=64) for t in range(PACK)]
 
-        def make_h(t, first, last, on_vector=False):
-            acc = psum_h.tile([P, BANK], F32, name="acc_h")[:, : last - first]
-            nc.tensor.matmul_mx(
-                out=acc, lhsT=w1_codes[:, t * P : (t + 1) * P].bitcast(FP8X4), lhsT_scale=w1_plane[:, t * P : (t + 1) * P],
-                rhs=xw_pick[:, first:last].bitcast(FP8X4), rhs_scale=xs_pick[:, first:last], start=True, stop=True,
-            )
+        def make_h(t, cuts, on_vector=False):
+            first, last = cuts[0], cuts[-1]
+            acc = next_bank(last - first)
+            for a, b in zip(cuts, cuts[1:]):
+                nc.tensor.matmul_mx(
+                    out=acc[:, a - first : b - first], lhsT=w1_codes[:, t * P : (t + 1) * P].bitcast(FP8X4),
+                    lhsT_scale=w1_plane[:, t * P : (t + 1) * P],
+                    rhs=xw_pick[:, a:b].bitcast(FP8X4), rhs_scale=xs_pick[:, a:b], start=True, stop=True,
+                )
             if on_vector:
                 nc.vector.tensor_scalar_max(h[t][:, first:last], acc, 0.0)
             else:
@@ -135,28 +144,22 @@ def tile_picked_sagecat_maxrelu_p_kernel(
             nc.vector.quantize_mx(out=codes[:].bitcast(FP8X4), scales=plane[:], in_=woven.rearrange("p v t -> p (v t)"))
             return codes, plane
 
-        for first in (0, 256):
-            make_h(0, first, first + 256)
-            make_h(1, first, first + 256)
-        make_h(0, 512, 768)
-        make_h(1, 512, 768, on_vector=True)
-        make_h(0, 768, 896)
-        make_h(0, 896, S)
-        make_h(1, 768, S)
+        for t in range(PACK):
+            make_h(t, CUTS[0:2])
+        for n in (1, 2):
+            make_h(0, CUTS[n : n + 2])
+            make_h(1, CUTS[n : n + 2])
+        make_h(0, CUTS[3:5], on_vector=True)
+        make_h(0, CUTS[4:6])
+        make_h(1, CUTS[3:6])
+        for t in (2, 3):
+            make_h(t, (CUTS[1], CUTS[3]))
+            make_h(t, CUTS[3:6])
 
         near = keep.tile([P, NEIGHBOURS, PACK, HALF], BF16, name="near_first", tag="near", align_bytes=64)
-        for d in range(NEIGHBOURS):
-            gather(near[:, d, 0, :], 0, pos_sb[d], 0, HALF, True)
-        gather(near[:, 2, 1, :], 1, pos_sb[2], 0, HALF, False)
-        make_h(2, 0, BANK)
-        make_h(2, BANK, S)
-        gather(near[:, 3, 1, :], 1, pos_sb[3], 0, HALF, False)
-        make_h(3, 0, BANK)
-        make_h(3, BANK, S)
-        for t in range(1, PACK):
+        for t in range(PACK):
             for d in range(NEIGHBOURS):
-                if t > 1 or d < 2:
-                    gather(near[:, d, t, :], t, pos_sb[d], 0, HALF, d < 2)
+                gather(near[:, d, t, :], t, pos_sb[d], 0, HALF, t == 0 or d < 2)
         pairs = keep.tile([P, 2, PACK, HALF], BF16, name="pairs", align_bytes=64)
         z_first = keep.tile([P, PACK, HALF], BF16, name="z_first", align_bytes=64)
         for t in (0, 2):
@@ -198,20 +201,20 @@ def tile_picked_sagecat_maxrelu_p_kernel(
 
         chunks = ((0, HALF), (HALF, HALF + QUARTER), (HALF + QUARTER, V))
         for (v0, v1), (codes, plane) in zip(chunks, z_codes):
-            acc = psum_out.tile([P, v1 - v0], F32, name="acc_out")
+            acc = next_bank(v1 - v0)
             centre_codes, centre_plane = c_codes[v0 // HALF]
             cols = slice(v0 % HALF, v0 % HALF + v1 - v0)
             nc.tensor.matmul_mx(
-                out=acc[:], lhsT=w2_codes[:].bitcast(FP8X4), lhsT_scale=w2_plane[:],
+                out=acc, lhsT=w2_codes[:].bitcast(FP8X4), lhsT_scale=w2_plane[:],
                 rhs=centre_codes[:, cols].bitcast(FP8X4), rhs_scale=centre_plane[:, cols], start=True, stop=False,
             )
             nc.tensor.matmul_mx(
-                out=acc[:], lhsT=w3_codes[:].bitcast(FP8X4), lhsT_scale=w3_plane[:],
+                out=acc, lhsT=w3_codes[:].bitcast(FP8X4), lhsT_scale=w3_plane[:],
                 rhs=codes[:].bitcast(FP8X4), rhs_scale=plane[:], start=False, stop=True,
             )
             result = keep.tile([P, v1 - v0], F32, name="result%d" % v0)
             if v1 == V:
-                nc.vector.tensor_scalar_max(result[:], acc[:], 0.0)
+                nc.vector.tensor_scalar_max(result[:], acc, 0.0)
             else:
-                nc.scalar.activation(result[:], acc[:], RELU)
+                nc.scalar.activation(result[:], acc, RELU)
             nc.sync.dma_start(out=out[:, v0:v1], in_=result[:])

@@ -27,6 +27,7 @@ NEIGHBOURS = 4
 HALF = V // 2
 QUARTER = V // 4
 BANKS = 8
+LAST_CUTS = (0, 128, 192, 256)
 CUTS = (0, 128, 384, 640, 896, S)
 
 
@@ -91,10 +92,9 @@ def tile_picked_sagecat_maxrelu_p_kernel(
         w1_pair = [keep.tile([P, 2, P, PACK], BF16, name="w1_pair%d" % n, align_bytes=64) for n in range(2)]
         early_rows, late_rows = [raw[:].rearrange("p j (m t) -> p m t j", t=PACK) for raw in (w1_early, w1_late)]
         by_place = [pair[:].rearrange("p t m j -> p m t j") for pair in w1_pair]
-        for n in range(2):
-            nc.scalar.copy(by_place[n][:, :, :, 0:2], early_rows[:, :, 2 * n : 2 * n + 2, :])
-        nc.scalar.copy(by_place[0][:, :, :, 2:4], late_rows[:, :, 0:2, :])
-        nc.gpsimd.tensor_scalar(by_place[1][:, :, :, 2:4], late_rows[:, :, 2:4, :], 1.0, 0.0, MULT, ADD)
+        for rows, j in ((early_rows, 0), (late_rows, 2)):
+            nc.scalar.copy(by_place[0][:, :, :, j : j + 2], rows[:, :, 0:2, :])
+            nc.gpsimd.tensor_scalar(by_place[1][:, :, :, j : j + 2], rows[:, :, 2:4, :], 1.0, 0.0, MULT, ADD)
         w1_codes = keep.tile([P, H], U32, name="w1_codes", tag="w1_codes_then_centres", align_bytes=64)
         w1_plane = keep.tile([P, H], U8, name="w1_plane", tag="w1_plane_then_centres", align_bytes=64)
         for n in range(2):
@@ -137,10 +137,10 @@ def tile_picked_sagecat_maxrelu_p_kernel(
         def weave_on_gpsimd(dst, slabs):
             nc.gpsimd.tensor_scalar(dst, slabs.rearrange("p t v -> p v t"), 1.0, 0.0, MULT, ADD)
 
-        def quantize(woven, name):
+        def quantize(woven, name, plane_tag=None):
             count = woven.shape[1]
             codes = keep.tile([P, count], U32, name=name + "_codes", align_bytes=64)
-            plane = keep.tile([P, count], U8, name=name + "_plane", align_bytes=64)
+            plane = keep.tile([P, count], U8, name=name + "_plane", tag=plane_tag or name + "_plane", align_bytes=64)
             nc.vector.quantize_mx(out=codes[:].bitcast(FP8X4), scales=plane[:], in_=woven.rearrange("p v t -> p (v t)"))
             return codes, plane
 
@@ -179,25 +179,28 @@ def tile_picked_sagecat_maxrelu_p_kernel(
         near = keep.tile([P, NEIGHBOURS, PACK, HALF], BF16, name="near_second", tag="near", align_bytes=64)
         for d in range(NEIGHBOURS):
             for t in range(PACK):
-                if (d, t) != (NEIGHBOURS - 1, PACK - 1):
+                if d < NEIGHBOURS - 1 or t < 2:
                     gather(near[:, d, t, :], t, pos_sb[d], HALF, V, d < 2 or (d, t) == (2, 0))
-        for v0 in (0, QUARTER):
-            gather(near[:, 3, 3, v0 : v0 + QUARTER], 3, pos_sb[3], HALF + v0, HALF + v0 + QUARTER, False)
+        for t, v0, v1 in ((2, 0, QUARTER), (3, 0, QUARTER), (2, QUARTER, HALF), (3, QUARTER, LAST_CUTS[2]), (3, LAST_CUTS[2], HALF)):
+            gather(near[:, 3, t, v0:v1], t, pos_sb[3], HALF + v0, HALF + v1, False)
         two = keep.tile([P, PACK, HALF], BF16, name="two", align_bytes=64)
         three = keep.tile([P, PACK, HALF], BF16, name="three", align_bytes=64)
-        z_second = keep.tile([P, PACK, HALF], BF16, name="z_second", align_bytes=64)
+        z_third = keep.tile([P, PACK, QUARTER], BF16, name="z_third", tag="z_third_then_last_plane", align_bytes=64)
+        z_fourth = keep.tile([P, PACK, QUARTER], BF16, name="z_fourth", align_bytes=64)
         nc.vector.tensor_tensor(two[:], near[:, 0], near[:, 1], MAX)
         z_codes = [quantize(z_woven[:, :HALF, :], "z0")]
         nc.vector.tensor_tensor(three[:], two[:], near[:, 2], MAX)
         c_codes = [quantize(c_woven[:, :HALF, :], "c0")]
-        nc.vector.tensor_tensor(z_second[:, 0:3, :], three[:, 0:3, :], near[:, 3, 0:3, :], MAX)
-        nc.vector.tensor_tensor(z_second[:, 3, :QUARTER], three[:, 3, :QUARTER], near[:, 3, 3, :QUARTER], MAX)
-        nc.vector.tensor_tensor(z_second[:, 3, QUARTER:], three[:, 3, QUARTER:], near[:, 3, 3, QUARTER:], MAX)
-        nc.vector.tensor_copy(*weave_views(z_woven[:, HALF : HALF + QUARTER, :], z_second[:, :, :QUARTER]))
-        nc.scalar.copy(*weave_views(z_woven[:, HALF + QUARTER :, :], z_second[:, :, QUARTER:]))
         c_codes.append(quantize(c_woven[:, HALF:, :], "c1"))
+        nc.vector.tensor_tensor(z_third[:], three[:, :, :QUARTER], near[:, 3, :, :QUARTER], MAX)
+        nc.vector.tensor_tensor(z_fourth[:, 0:3, :], three[:, 0:3, QUARTER:], near[:, 3, 0:3, QUARTER:], MAX)
+        for v0, v1 in zip(LAST_CUTS[1:], LAST_CUTS[2:]):
+            nc.vector.tensor_tensor(z_fourth[:, 3, v0 - QUARTER : v1 - QUARTER], three[:, 3, v0:v1], near[:, 3, 3, v0:v1], MAX)
+        nc.scalar.copy(*weave_views(z_woven[:, HALF : HALF + QUARTER, :], z_third[:]))
+        for v0, v1 in zip(LAST_CUTS[1:], LAST_CUTS[2:]):
+            nc.vector.tensor_copy(*weave_views(z_woven[:, HALF + v0 : HALF + v1, :], z_fourth[:, :, v0 - QUARTER : v1 - QUARTER]))
         z_codes.append(quantize(z_woven[:, HALF : HALF + QUARTER, :], "z1"))
-        z_codes.append(quantize(z_woven[:, HALF + QUARTER :, :], "z2"))
+        z_codes.append(quantize(z_woven[:, HALF + QUARTER :, :], "z2", "z_third_then_last_plane"))
 
         chunks = ((0, HALF), (HALF, HALF + QUARTER), (HALF + QUARTER, V))
         for (v0, v1), (codes, plane) in zip(chunks, z_codes):

@@ -156,46 +156,58 @@ def tile_picked_sagecat_maxrelu_p_kernel(
             make_h(t, (CUTS[1], CUTS[3]))
             make_h(t, CUTS[3:6])
 
-        near = keep.tile([P, NEIGHBOURS, PACK, HALF], BF16, name="near_first", tag="near", align_bytes=64)
-        for t in range(PACK):
+        ends = keep.tile([P, 2, 2, PACK, HALF], BF16, name="ends", align_bytes=64)
+        near0 = keep.tile([P, NEIGHBOURS, V], BF16, name="near0", align_bytes=64)
+        for d in range(NEIGHBOURS):
+            gather(near0[:, d, :], 0, pos_sb[d], 0, V, True)
+        low, high = [near0[:, d : d + 2, :].rearrange("p s (h v) -> p h s v", h=2) for d in (0, 2)]
+        nc.vector.tensor_tensor(ends[:, :, :, 0, :], low, high, MAX)
+
+        c_woven = keep.tile([P, V, PACK], BF16, name="c_woven", align_bytes=64)
+        c_slabs = keep.tile([P, PACK, V], BF16, name="c_slabs", tag="w1_codes_then_centres", align_bytes=64)
+        for t in (0, 1):
+            gather(c_slabs[:, t, :], t, cen_sb, 0, V, False)
+        for v0 in (0, HALF):
+            for t in (2, 3):
+                gather(c_slabs[:, t, v0 : v0 + HALF], t, cen_sb, v0, v0 + HALF, False)
+            weave_on_gpsimd(c_woven[:, v0 : v0 + HALF, :], c_slabs[:, :, v0 : v0 + HALF])
+
+        near = keep.tile([P, 2, PACK - 1, HALF], BF16, name="near_first", tag="near", align_bytes=64)
+        for t in range(1, PACK):
             for d in range(NEIGHBOURS):
-                gather(near[:, d, t, :], t, pos_sb[d], 0, HALF, t == 0 or d < 2)
-        pairs = keep.tile([P, 2, PACK, HALF], BF16, name="pairs", align_bytes=64)
-        z_first = keep.tile([P, PACK, HALF], BF16, name="z_first", align_bytes=64)
-        for t in (0, 2):
-            nc.vector.tensor_tensor(pairs[:, :, t : t + 2, :], near[:, 0:2, t : t + 2, :], near[:, 2:4, t : t + 2, :], MAX)
-        for t in (0, 2):
-            nc.vector.tensor_tensor(z_first[:, t : t + 2, :], pairs[:, 0, t : t + 2, :], pairs[:, 1, t : t + 2, :], MAX)
+                dst = near[:, d, t - 1, :] if d < 2 else ends[:, 1, d - 2, t, :]
+                gather(dst, t, pos_sb[d], 0, HALF, t == 1 or d < 2)
+        quarters = (slice(0, QUARTER), slice(QUARTER, HALF))
+        for cols in quarters:
+            nc.vector.tensor_tensor(ends[:, 0, :, 1:, cols], near[:, :, :, cols], ends[:, 1, :, 1:, cols], MAX)
+        c_codes = [quantize(c_woven[:, :HALF, :], "c0")]
+        z_first = keep.tile([P, PACK, HALF], BF16, name="z_first", tag="z_first_then_two", align_bytes=64)
+        for cols in quarters:
+            nc.vector.tensor_tensor(z_first[:, :, cols], ends[:, 0, 0, :, cols], ends[:, 0, 1, :, cols], MAX)
         z_woven = keep.tile([P, V, PACK], BF16, name="z_woven", align_bytes=64)
         weave_on_gpsimd(z_woven[:, :HALF, :], z_first[:])
 
-        c_woven = keep.tile([P, V, PACK], BF16, name="c_woven", align_bytes=64)
-        for v0, tag in ((0, "w1_codes_then_centres"), (HALF, "w1_plane_then_centres")):
-            c_slabs = keep.tile([P, PACK, HALF], BF16, name="c_slabs%d" % v0, tag=tag, align_bytes=64)
-            for t in range(PACK):
-                gather(c_slabs[:, t, :], t, cen_sb, v0, v0 + HALF, False)
-            weave_on_gpsimd(c_woven[:, v0 : v0 + HALF, :], c_slabs[:])
-
-        near = keep.tile([P, NEIGHBOURS, PACK, HALF], BF16, name="near_second", tag="near", align_bytes=64)
-        for d in range(NEIGHBOURS):
-            for t in range(PACK):
-                if d < NEIGHBOURS - 1 or t < 2:
-                    gather(near[:, d, t, :], t, pos_sb[d], HALF, V, d < 2 or (d, t) == (2, 0))
-        for t, v0, v1 in ((2, 0, QUARTER), (3, 0, QUARTER), (2, QUARTER, HALF), (3, QUARTER, LAST_CUTS[2]), (3, LAST_CUTS[2], HALF)):
-            gather(near[:, 3, t, v0:v1], t, pos_sb[3], HALF + v0, HALF + v1, False)
-        two = keep.tile([P, PACK, HALF], BF16, name="two", align_bytes=64)
-        three = keep.tile([P, PACK, HALF], BF16, name="three", align_bytes=64)
+        first = keep.tile([P, PACK - 1, HALF], BF16, name="near_second", tag="near", align_bytes=64)
+        middle = keep.tile([P, 2, PACK - 1, HALF], BF16, name="middle", tag="w1_plane_then_centres", align_bytes=64)
+        three, fourth = ends[:, 1, 0], ends[:, 1, 1]
+        for t in range(1, PACK):
+            gather(first[:, t - 1, :], t, pos_sb[0], HALF, V, True)
+        for d in (1, 2):
+            for t in range(1, PACK):
+                gather(middle[:, d - 1, t - 1, :], t, pos_sb[d], HALF, V, False)
+        for t, v0, v1 in ((1, 0, HALF), (2, 0, QUARTER), (3, 0, QUARTER), (2, QUARTER, HALF), (3, QUARTER, LAST_CUTS[2]), (3, LAST_CUTS[2], HALF)):
+            gather(fourth[:, t, v0:v1], t, pos_sb[3], HALF + v0, HALF + v1, False)
+        two = keep.tile([P, PACK - 1, HALF], BF16, name="two", tag="z_first_then_two", align_bytes=64)
         z_third = keep.tile([P, PACK, QUARTER], BF16, name="z_third", tag="z_third_then_last_plane", align_bytes=64)
         z_fourth = keep.tile([P, PACK, QUARTER], BF16, name="z_fourth", align_bytes=64)
-        nc.vector.tensor_tensor(two[:], near[:, 0], near[:, 1], MAX)
+        nc.vector.tensor_tensor(two[:], first[:], middle[:, 0], MAX)
         z_codes = [quantize(z_woven[:, :HALF, :], "z0")]
-        nc.vector.tensor_tensor(three[:], two[:], near[:, 2], MAX)
-        c_codes = [quantize(c_woven[:, :HALF, :], "c0")]
+        nc.vector.tensor_tensor(three[:, 1:, :], two[:], middle[:, 1], MAX)
         c_codes.append(quantize(c_woven[:, HALF:, :], "c1"))
-        nc.vector.tensor_tensor(z_third[:], three[:, :, :QUARTER], near[:, 3, :, :QUARTER], MAX)
-        nc.vector.tensor_tensor(z_fourth[:, 0:3, :], three[:, 0:3, QUARTER:], near[:, 3, 0:3, QUARTER:], MAX)
+        nc.vector.tensor_tensor(z_third[:], three[:, :, :QUARTER], fourth[:, :, :QUARTER], MAX)
+        nc.vector.tensor_tensor(z_fourth[:, 0:3, :], three[:, 0:3, QUARTER:], fourth[:, 0:3, QUARTER:], MAX)
         for v0, v1 in zip(LAST_CUTS[1:], LAST_CUTS[2:]):
-            nc.vector.tensor_tensor(z_fourth[:, 3, v0 - QUARTER : v1 - QUARTER], three[:, 3, v0:v1], near[:, 3, 3, v0:v1], MAX)
+            nc.vector.tensor_tensor(z_fourth[:, 3, v0 - QUARTER : v1 - QUARTER], three[:, 3, v0:v1], fourth[:, 3, v0:v1], MAX)
         nc.scalar.copy(*weave_views(z_woven[:, HALF : HALF + QUARTER, :], z_third[:]))
         for v0, v1 in zip(LAST_CUTS[1:], LAST_CUTS[2:]):
             nc.vector.tensor_copy(*weave_views(z_woven[:, HALF + v0 : HALF + v1, :], z_fourth[:, :, v0 - QUARTER : v1 - QUARTER]))

@@ -27,6 +27,7 @@ NEIGHBOURS = 4
 HALF = V // 2
 QUARTER = V // 4
 BANKS = 8
+SCALAR_PLACES = 80
 LAST_CUTS = (0, 128, 192, 256)
 CUTS = (0, 128, 384, 640, 896, S)
 
@@ -51,6 +52,7 @@ def tile_picked_sagecat_maxrelu_p_kernel(
     with ExitStack() as ctx:
         lists = ctx.enter_context(tc.tile_pool(name="lists", bufs=1))
         keep = ctx.enter_context(tc.tile_pool(name="keep", bufs=1))
+        shared = ctx.enter_context(tc.tile_pool(name="shared", bufs=1))
         psum = ctx.enter_context(tc.psum_pool(name="psum", bufs=1))
         taken = []
 
@@ -89,19 +91,15 @@ def tile_picked_sagecat_maxrelu_p_kernel(
         xs_pick = keep.tile([P, S], U8, name="xs_pick", align_bytes=64)
         nc.vector.tensor_copy(xs_pick[:], xs_all[:].indirect(offs_sb[:]))
 
-        w1_pair = [keep.tile([P, 2, P, PACK], BF16, name="w1_pair%d" % n, align_bytes=64) for n in range(2)]
-        early_rows, late_rows = [raw[:].rearrange("p j (m t) -> p m t j", t=PACK) for raw in (w1_early, w1_late)]
-        by_place = [pair[:].rearrange("p t m j -> p m t j") for pair in w1_pair]
-        for rows, j in ((early_rows, 0), (late_rows, 2)):
-            nc.scalar.copy(by_place[0][:, :, :, j : j + 2], rows[:, :, 0:2, :])
-            nc.gpsimd.tensor_scalar(by_place[1][:, :, :, j : j + 2], rows[:, :, 2:4, :], 1.0, 0.0, MULT, ADD)
+        w1_rounded = keep.tile([P, PACK, P, PACK], BF16, name="w1_rounded", align_bytes=64)
+        by_place = w1_rounded[:].rearrange("p t m j -> p m t j")
+        for raw, j in ((w1_early, 0), (w1_late, 2)):
+            rows = raw[:].rearrange("p j (m t) -> p m t j", t=PACK)
+            nc.scalar.copy(by_place[:, :SCALAR_PLACES, :, j : j + 2], rows[:, :SCALAR_PLACES])
+            nc.gpsimd.tensor_scalar(by_place[:, SCALAR_PLACES:, :, j : j + 2], rows[:, SCALAR_PLACES:], 1.0, 0.0, MULT, ADD)
         w1_codes = keep.tile([P, H], U32, name="w1_codes", tag="w1_codes_then_centres", align_bytes=64)
         w1_plane = keep.tile([P, H], U8, name="w1_plane", tag="w1_plane_then_centres", align_bytes=64)
-        for n in range(2):
-            cols = slice(2 * n * P, (2 * n + 2) * P)
-            nc.vector.quantize_mx(
-                out=w1_codes[:, cols].bitcast(FP8X4), scales=w1_plane[:, cols], in_=w1_pair[n][:].rearrange("p t m j -> p (t m j)")
-            )
+        nc.vector.quantize_mx(out=w1_codes[:].bitcast(FP8X4), scales=w1_plane[:], in_=w1_rounded[:].rearrange("p t m j -> p (t m j)"))
 
         xw_window = xw_all[:].bitcast(U32)
         xw_pick = keep.tile([P, S], U32, name="xw_pick", align_bytes=64)
@@ -137,10 +135,11 @@ def tile_picked_sagecat_maxrelu_p_kernel(
         def weave_on_gpsimd(dst, slabs):
             nc.gpsimd.tensor_scalar(dst, slabs.rearrange("p t v -> p v t"), 1.0, 0.0, MULT, ADD)
 
-        def quantize(woven, name, plane_tag=None):
+        def quantize(woven, name, plane=None):
             count = woven.shape[1]
             codes = keep.tile([P, count], U32, name=name + "_codes", align_bytes=64)
-            plane = keep.tile([P, count], U8, name=name + "_plane", tag=plane_tag or name + "_plane", align_bytes=64)
+            if plane is None:
+                plane = keep.tile([P, count], U8, name=name + "_plane", align_bytes=64)
             nc.vector.quantize_mx(out=codes[:].bitcast(FP8X4), scales=plane[:], in_=woven.rearrange("p v t -> p (v t)"))
             return codes, plane
 
@@ -157,13 +156,13 @@ def tile_picked_sagecat_maxrelu_p_kernel(
             make_h(t, CUTS[3:6])
 
         ends = keep.tile([P, 2, 2, PACK, HALF], BF16, name="ends", align_bytes=64)
-        near0 = keep.tile([P, NEIGHBOURS, V], BF16, name="near0", align_bytes=64)
+        near0 = keep.tile([P, NEIGHBOURS, V], BF16, name="near0", tag="near0_then_centres", align_bytes=64)
         for d in range(NEIGHBOURS):
             gather(near0[:, d, :], 0, pos_sb[d], 0, V, True)
         low, high = [near0[:, d : d + 2, :].rearrange("p s (h v) -> p h s v", h=2) for d in (0, 2)]
         nc.vector.tensor_tensor(ends[:, :, :, 0, :], low, high, MAX)
 
-        c_woven = keep.tile([P, V, PACK], BF16, name="c_woven", align_bytes=64)
+        c_woven = keep.tile([P, V, PACK], BF16, name="c_woven", tag="near0_then_centres", align_bytes=64)
         c_slabs = keep.tile([P, PACK, V], BF16, name="c_slabs", tag="w1_codes_then_centres", align_bytes=64)
         for t in (0, 1):
             gather(c_slabs[:, t, :], t, cen_sb, 0, V, False)
@@ -180,8 +179,7 @@ def tile_picked_sagecat_maxrelu_p_kernel(
         quarters = (slice(0, QUARTER), slice(QUARTER, HALF))
         for cols in quarters:
             nc.vector.tensor_tensor(ends[:, 0, :, 1:, cols], near[:, :, :, cols], ends[:, 1, :, 1:, cols], MAX)
-        c_codes = [quantize(c_woven[:, :HALF, :], "c0")]
-        z_first = keep.tile([P, PACK, HALF], BF16, name="z_first", tag="z_first_then_two", align_bytes=64)
+        z_first = shared.tile([P, PACK, HALF], BF16, name="z_first", offset=0, align_bytes=64)
         for cols in quarters:
             nc.vector.tensor_tensor(z_first[:, :, cols], ends[:, 0, 0, :, cols], ends[:, 0, 1, :, cols], MAX)
         z_woven = keep.tile([P, V, PACK], BF16, name="z_woven", align_bytes=64)
@@ -197,13 +195,14 @@ def tile_picked_sagecat_maxrelu_p_kernel(
                 gather(middle[:, d - 1, t - 1, :], t, pos_sb[d], HALF, V, False)
         for t, v0, v1 in ((1, 0, HALF), (2, 0, QUARTER), (3, 0, QUARTER), (2, QUARTER, HALF), (3, QUARTER, LAST_CUTS[2]), (3, LAST_CUTS[2], HALF)):
             gather(fourth[:, t, v0:v1], t, pos_sb[3], HALF + v0, HALF + v1, False)
-        two = keep.tile([P, PACK - 1, HALF], BF16, name="two", tag="z_first_then_two", align_bytes=64)
+        two = shared.tile([P, PACK - 1, HALF], BF16, name="two", offset=3 * HALF, align_bytes=64)
         z_third = keep.tile([P, PACK, QUARTER], BF16, name="z_third", tag="z_third_then_last_plane", align_bytes=64)
         z_fourth = keep.tile([P, PACK, QUARTER], BF16, name="z_fourth", align_bytes=64)
         nc.vector.tensor_tensor(two[:], first[:], middle[:, 0], MAX)
-        z_codes = [quantize(z_woven[:, :HALF, :], "z0")]
+        planes = [shared.tile([P, HALF], U8, name="late_plane%d" % n, offset=n * HALF, align_bytes=64) for n in range(3)]
+        z_codes = [quantize(z_woven[:, :HALF, :], "z0", planes[0])]
         nc.vector.tensor_tensor(three[:, 1:, :], two[:], middle[:, 1], MAX)
-        c_codes.append(quantize(c_woven[:, HALF:, :], "c1"))
+        c_codes = [quantize(c_woven[:, :HALF, :], "c0", planes[1])]
         nc.vector.tensor_tensor(z_third[:], three[:, :, :QUARTER], fourth[:, :, :QUARTER], MAX)
         nc.vector.tensor_tensor(z_fourth[:, 0:3, :], three[:, 0:3, QUARTER:], fourth[:, 0:3, QUARTER:], MAX)
         for v0, v1 in zip(LAST_CUTS[1:], LAST_CUTS[2:]):
@@ -211,8 +210,10 @@ def tile_picked_sagecat_maxrelu_p_kernel(
         nc.scalar.copy(*weave_views(z_woven[:, HALF : HALF + QUARTER, :], z_third[:]))
         for v0, v1 in zip(LAST_CUTS[1:], LAST_CUTS[2:]):
             nc.vector.tensor_copy(*weave_views(z_woven[:, HALF + v0 : HALF + v1, :], z_fourth[:, :, v0 - QUARTER : v1 - QUARTER]))
+        c_codes.append(quantize(c_woven[:, HALF:, :], "c1", planes[2]))
         z_codes.append(quantize(z_woven[:, HALF : HALF + QUARTER, :], "z1"))
-        z_codes.append(quantize(z_woven[:, HALF + QUARTER :, :], "z2", "z_third_then_last_plane"))
+        last_plane = keep.tile([P, QUARTER], U8, name="last_plane", tag="z_third_then_last_plane", align_bytes=64)
+        z_codes.append(quantize(z_woven[:, HALF + QUARTER :, :], "z2", last_plane))
 
         chunks = ((0, HALF), (HALF, HALF + QUARTER), (HALF + QUARTER, V))
         for (v0, v1), (codes, plane) in zip(chunks, z_codes):

@@ -28,7 +28,6 @@ HALF = V // 2
 QUARTER = V // 4
 BANKS = 8
 SCALAR_PLACES = 80
-LAST_CUTS = (0, 128, 192, 256)
 CUTS = (0, 128, 384, 640, 896, S)
 
 
@@ -53,6 +52,7 @@ def tile_picked_sagecat_maxrelu_p_kernel(
         lists = ctx.enter_context(tc.tile_pool(name="lists", bufs=1))
         keep = ctx.enter_context(tc.tile_pool(name="keep", bufs=1))
         shared = ctx.enter_context(tc.tile_pool(name="shared", bufs=1))
+        after_middle = ctx.enter_context(tc.tile_pool(name="after_middle", bufs=1))
         psum = ctx.enter_context(tc.psum_pool(name="psum", bufs=1))
         taken = []
 
@@ -98,7 +98,7 @@ def tile_picked_sagecat_maxrelu_p_kernel(
             nc.scalar.copy(by_place[:, :SCALAR_PLACES, :, j : j + 2], rows[:, :SCALAR_PLACES])
             nc.gpsimd.tensor_scalar(by_place[:, SCALAR_PLACES:, :, j : j + 2], rows[:, SCALAR_PLACES:], 1.0, 0.0, MULT, ADD)
         w1_codes = keep.tile([P, H], U32, name="w1_codes", tag="w1_codes_then_centres", align_bytes=64)
-        w1_plane = keep.tile([P, H], U8, name="w1_plane", tag="w1_plane_then_centres", align_bytes=64)
+        w1_plane = after_middle.tile([P, H], U8, name="w1_plane", offset=0, align_bytes=64)
         nc.vector.quantize_mx(out=w1_codes[:].bitcast(FP8X4), scales=w1_plane[:], in_=w1_rounded[:].rearrange("p t m j -> p (t m j)"))
 
         xw_window = xw_all[:].bitcast(U32)
@@ -186,31 +186,32 @@ def tile_picked_sagecat_maxrelu_p_kernel(
         weave_on_gpsimd(z_woven[:, :HALF, :], z_first[:])
 
         first = keep.tile([P, PACK - 1, HALF], BF16, name="near_second", tag="near", align_bytes=64)
-        middle = keep.tile([P, 2, PACK - 1, HALF], BF16, name="middle", tag="w1_plane_then_centres", align_bytes=64)
+        middle = after_middle.tile([P, 2, PACK - 1, HALF], BF16, name="middle", offset=0, align_bytes=64)
         three, fourth = ends[:, 1, 0], ends[:, 1, 1]
         for t in range(1, PACK):
             gather(first[:, t - 1, :], t, pos_sb[0], HALF, V, True)
         for d in (1, 2):
             for t in range(1, PACK):
                 gather(middle[:, d - 1, t - 1, :], t, pos_sb[d], HALF, V, False)
-        for t, v0, v1 in ((1, 0, HALF), (2, 0, QUARTER), (3, 0, QUARTER), (2, QUARTER, HALF), (3, QUARTER, LAST_CUTS[2]), (3, LAST_CUTS[2], HALF)):
-            gather(fourth[:, t, v0:v1], t, pos_sb[3], HALF + v0, HALF + v1, False)
-        two = shared.tile([P, PACK - 1, HALF], BF16, name="two", offset=3 * HALF, align_bytes=64)
+        for cols in quarters:
+            for t in range(1, PACK):
+                gather(fourth[:, t, cols], t, pos_sb[3], HALF + cols.start, HALF + cols.stop, False)
+        two = shared.tile([P, PACK - 1, HALF], BF16, name="two", offset=HALF, align_bytes=64)
         z_third = keep.tile([P, PACK, QUARTER], BF16, name="z_third", tag="z_third_then_last_plane", align_bytes=64)
         z_fourth = keep.tile([P, PACK, QUARTER], BF16, name="z_fourth", align_bytes=64)
         nc.vector.tensor_tensor(two[:], first[:], middle[:, 0], MAX)
-        planes = [shared.tile([P, HALF], U8, name="late_plane%d" % n, offset=n * HALF, align_bytes=64) for n in range(3)]
+        planes = [shared.tile([P, HALF], U8, name="z0_plane", offset=0, align_bytes=64)]
+        planes += [after_middle.tile([P, HALF], U8, name="c_plane%d" % n, offset=n * HALF, align_bytes=64) for n in range(2)]
         z_codes = [quantize(z_woven[:, :HALF, :], "z0", planes[0])]
-        nc.vector.tensor_tensor(three[:, 1:, :], two[:], middle[:, 1], MAX)
-        c_codes = [quantize(c_woven[:, :HALF, :], "c0", planes[1])]
+        for cols in quarters:
+            nc.vector.tensor_tensor(three[:, 1:, cols], two[:, :, cols], middle[:, 1, :, cols], MAX)
         nc.vector.tensor_tensor(z_third[:], three[:, :, :QUARTER], fourth[:, :, :QUARTER], MAX)
         nc.vector.tensor_tensor(z_fourth[:, 0:3, :], three[:, 0:3, QUARTER:], fourth[:, 0:3, QUARTER:], MAX)
-        for v0, v1 in zip(LAST_CUTS[1:], LAST_CUTS[2:]):
-            nc.vector.tensor_tensor(z_fourth[:, 3, v0 - QUARTER : v1 - QUARTER], three[:, 3, v0:v1], fourth[:, 3, v0:v1], MAX)
+        c_codes = [quantize(c_woven[:, :HALF, :], "c0", planes[1])]
+        nc.vector.tensor_tensor(z_fourth[:, 3, :], three[:, 3, QUARTER:], fourth[:, 3, QUARTER:], MAX)
         nc.scalar.copy(*weave_views(z_woven[:, HALF : HALF + QUARTER, :], z_third[:]))
-        for v0, v1 in zip(LAST_CUTS[1:], LAST_CUTS[2:]):
-            nc.vector.tensor_copy(*weave_views(z_woven[:, HALF + v0 : HALF + v1, :], z_fourth[:, :, v0 - QUARTER : v1 - QUARTER]))
         c_codes.append(quantize(c_woven[:, HALF:, :], "c1", planes[2]))
+        nc.vector.tensor_copy(*weave_views(z_woven[:, HALF + QUARTER :, :], z_fourth[:]))
         z_codes.append(quantize(z_woven[:, HALF : HALF + QUARTER, :], "z1"))
         last_plane = keep.tile([P, QUARTER], U8, name="last_plane", tag="z_third_then_last_plane", align_bytes=64)
         z_codes.append(quantize(z_woven[:, HALF + QUARTER :, :], "z2", last_plane))

@@ -179,11 +179,15 @@ def tile_picked_sagecat_maxrelu_p_kernel(
         quarters = (slice(0, QUARTER), slice(QUARTER, HALF))
         for cols in quarters:
             nc.vector.tensor_tensor(ends[:, 0, :, 1:, cols], near[:, :, :, cols], ends[:, 1, :, 1:, cols], MAX)
-        z_first = shared.tile([P, PACK, HALF], BF16, name="z_first", offset=0, align_bytes=64)
-        for cols in quarters:
-            nc.vector.tensor_tensor(z_first[:, :, cols], ends[:, 0, 0, :, cols], ends[:, 0, 1, :, cols], MAX)
+        z_quarters = [
+            shared.tile([P, PACK, QUARTER], BF16, name="z_quarter0", offset=0, align_bytes=64),
+            keep.tile([P, PACK, QUARTER], BF16, name="z_quarter1", align_bytes=64),
+        ]
+        for cols, z_quarter in zip(quarters, z_quarters):
+            nc.vector.tensor_tensor(z_quarter[:], ends[:, 0, 0, :, cols], ends[:, 0, 1, :, cols], MAX)
         z_woven = keep.tile([P, V, PACK], BF16, name="z_woven", align_bytes=64)
-        weave_on_gpsimd(z_woven[:, :HALF, :], z_first[:])
+        for cols, z_quarter in zip(quarters, z_quarters):
+            weave_on_gpsimd(z_woven[:, cols, :], z_quarter[:])
 
         first = keep.tile([P, PACK - 1, HALF], BF16, name="near_second", tag="near", align_bytes=64)
         middle = after_middle.tile([P, 2, PACK - 1, HALF], BF16, name="middle", offset=0, align_bytes=64)
@@ -202,12 +206,12 @@ def tile_picked_sagecat_maxrelu_p_kernel(
         nc.vector.tensor_tensor(two[:], first[:], middle[:, 0], MAX)
         planes = [shared.tile([P, HALF], U8, name="z0_plane", offset=0, align_bytes=64)]
         planes += [after_middle.tile([P, HALF], U8, name="c_plane%d" % n, offset=n * HALF, align_bytes=64) for n in range(2)]
-        z_codes = [quantize(z_woven[:, :HALF, :], "z0", planes[0])]
+        c_codes = [quantize(c_woven[:, :HALF, :], "c0", planes[0])]
         for cols in quarters:
             nc.vector.tensor_tensor(three[:, 1:, cols], two[:, :, cols], middle[:, 1, :, cols], MAX)
         nc.vector.tensor_tensor(z_third[:], three[:, :, :QUARTER], fourth[:, :, :QUARTER], MAX)
         nc.vector.tensor_tensor(z_fourth[:, 0:3, :], three[:, 0:3, QUARTER:], fourth[:, 0:3, QUARTER:], MAX)
-        c_codes = [quantize(c_woven[:, :HALF, :], "c0", planes[1])]
+        z_codes = [quantize(z_woven[:, :HALF, :], "z0", planes[1])]
         nc.vector.tensor_tensor(z_fourth[:, 3, :], three[:, 3, QUARTER:], fourth[:, 3, QUARTER:], MAX)
         nc.scalar.copy(*weave_views(z_woven[:, HALF : HALF + QUARTER, :], z_third[:]))
         c_codes.append(quantize(c_woven[:, HALF:, :], "c1", planes[2]))

@@ -164,18 +164,19 @@ def tile_picked_sagecat_maxrelu_p_kernel(
 
         c_woven = keep.tile([P, V, PACK], BF16, name="c_woven", tag="near0_then_centres", align_bytes=64)
         c_slabs = keep.tile([P, PACK, V], BF16, name="c_slabs", tag="w1_codes_then_centres", align_bytes=64)
-        for t in (0, 1):
+        for t in range(PACK):
             gather(c_slabs[:, t, :], t, cen_sb, 0, V, False)
-        for v0 in (0, HALF):
-            for t in (2, 3):
-                gather(c_slabs[:, t, v0 : v0 + HALF], t, cen_sb, v0, v0 + HALF, False)
-            weave_on_gpsimd(c_woven[:, v0 : v0 + HALF, :], c_slabs[:, :, v0 : v0 + HALF])
+        weave_on_gpsimd(c_woven[:], c_slabs[:])
 
         near = keep.tile([P, 2, PACK - 1, HALF], BF16, name="near_first", tag="near", align_bytes=64)
         for t in range(1, PACK):
             for d in range(NEIGHBOURS):
                 dst = near[:, d, t - 1, :] if d < 2 else ends[:, 1, d - 2, t, :]
-                gather(dst, t, pos_sb[d], 0, HALF, t == 1 or d < 2)
+                if (t, d) == (3, 1):
+                    gather(dst[:, :QUARTER], t, pos_sb[d], 0, QUARTER, True)
+                    gather(dst[:, QUARTER:], t, pos_sb[d], QUARTER, HALF, False)
+                else:
+                    gather(dst, t, pos_sb[d], 0, HALF, t == 1 or d < 2)
         quarters = (slice(0, QUARTER), slice(QUARTER, HALF))
         for cols in quarters:
             nc.vector.tensor_tensor(ends[:, 0, :, 1:, cols], near[:, :, :, cols], ends[:, 1, :, 1:, cols], MAX)

@@ -27,7 +27,7 @@ NEIGHBOURS = 4
 HALF = V // 2
 QUARTER = V // 4
 BANKS = 8
-SCALAR_PLACES = 80
+SCALAR_PLACES = 68
 CUTS = (0, 128, 384, 640, 896, S)
 
 

from contextlib import ExitStack

import concourse.mybir as mybir

K, T, S, V, H, N = 512, 2048, 1024, 512, 512, 128
FLOPS = 2 * K * H * S + 2 * 2 * H * N * V

F32 = mybir.dt.float32
BF16 = mybir.dt.bfloat16
I32 = mybir.dt.int32
U32 = mybir.dt.uint32
U16 = mybir.dt.uint16
U8 = mybir.dt.uint8
FP8X4 = mybir.dt.float8_e4m3fn_x4
RELU = mybir.ActivationFunctionType.Relu
COPY = mybir.ActivationFunctionType.Copy
MAX = mybir.AluOpType.max
MULT = mybir.AluOpType.mult
ADD = mybir.AluOpType.add

P = 128
PACK = 4
QUADRANT = 32
BANK = 512
LIST_ROWS = 16
NEIGHBOURS = 4
HALF = V // 2
QUARTER = V // 4
BANKS = 8
SCALAR_PLACES = 68
CUTS = (0, 128, 384, 640, 896, S)


def load_scale_rows(nc, plane, scales):
    for q in range(P // QUADRANT):
        nc.sync.dma_start(out=plane[QUADRANT * q : QUADRANT * q + 4, :].bitcast(I32), in_=scales[0, 4 * q : 4 * q + 4, :].bitcast(I32))


def words_of(dram_words):
    return dram_words[0].rearrange("p n t -> p (n t)").bitcast(I32)


def entries(offsets, first, last):
    return offsets[:, first // LIST_ROWS : last // LIST_ROWS]


def tile_picked_sagecat_maxrelu_p_kernel(
    tc, x_words, x_scales, w1, w2_words, w2_scales, w3_words, w3_scales, offs, cen, pos1, pos2, pos3, pos4, out
):
    nc = tc.nc
    with ExitStack() as ctx:
        lists = ctx.enter_context(tc.tile_pool(name="lists", bufs=1))
        keep = ctx.enter_context(tc.tile_pool(name="keep", bufs=1))
        shared = ctx.enter_context(tc.tile_pool(name="shared", bufs=1))
        after_middle = ctx.enter_context(tc.tile_pool(name="after_middle", bufs=1))
        psum = ctx.enter_context(tc.psum_pool(name="psum", bufs=1))
        taken = []

        def next_bank(count):
            taken.append(count)
            return psum.tile([P, BANK], F32, name="acc", tag="bank%d" % (len(taken) % BANKS))[:, :count]

        xs_all = keep.tile([P, T], U8, name="xs_all", align_bytes=64)
        nc.vector.memset(xs_all[:, : T // 2].bitcast(I32), 0)
        nc.gpsimd.memset(xs_all[:, T // 2 :].bitcast(I32), 0)
        offs_sb = lists.tile([P, S // LIST_ROWS], U16, name="offs_sb")
        pos_sb = [lists.tile([P, V // LIST_ROWS], U16, name="pos_sb%d" % d) for d in range(NEIGHBOURS)]
        cen_sb = lists.tile([P, V // LIST_ROWS], U16, name="cen_sb")
        w1_rows = w1.rearrange("(p j) c -> p j c", j=PACK)
        w1_early = keep.tile([P, 2, H], F32, name="w1_early")
        w1_late = keep.tile([P, 2, H], F32, name="w1_late")
        xw_all = keep.tile([P, T], I32, name="xw_all", align_bytes=64)
        nc.sync.dma_start(out=w1_early[:], in_=w1_rows[:, 0:2, :])
        nc.sync.dma_start(offs_sb[:], offs)
        load_scale_rows(nc, xs_all, x_scales)
        nc.sync.dma_start(out=w1_late[:], in_=w1_rows[:, 2:4, :])
        nc.sync.dma_start(out=xw_all[:], in_=words_of(x_words))
        for offsets, pos in zip(pos_sb, (pos1, pos2, pos3, pos4)):
            nc.sync.dma_start(offsets[:], pos)
        nc.sync.dma_start(cen_sb[:], cen)

        w2_codes = keep.tile([P, N], I32, name="w2_codes", align_bytes=64)
        w3_codes = keep.tile([P, N], I32, name="w3_codes", align_bytes=64)
        w2_plane = keep.tile([P, N], U8, name="w2_plane", align_bytes=64)
        w3_plane = keep.tile([P, N], U8, name="w3_plane", align_bytes=64)
        for codes, plane, words, scales in ((w3_codes, w3_plane, w3_words, w3_scales), (w2_codes, w2_plane, w2_words, w2_scales)):
            nc.sync.dma_start(out=codes[:], in_=words_of(words))
            nc.gpsimd.memset(plane[:].bitcast(I32), 0)
            load_scale_rows(nc, plane, scales)

        xs_pick = keep.tile([P, S], U8, name="xs_pick", align_bytes=64)
        nc.vector.tensor_copy(xs_pick[:], xs_all[:].indirect(offs_sb[:]))

        w1_rounded = keep.tile([P, PACK, P, PACK], BF16, name="w1_rounded", align_bytes=64)
        by_place = w1_rounded[:].rearrange("p t m j -> p m t j")
        for raw, j in ((w1_early, 0), (w1_late, 2)):
            rows = raw[:].rearrange("p j (m t) -> p m t j", t=PACK)
            nc.scalar.copy(by_place[:, :SCALAR_PLACES, :, j : j + 2], rows[:, :SCALAR_PLACES])
            nc.gpsimd.tensor_scalar(by_place[:, SCALAR_PLACES:, :, j : j + 2], rows[:, SCALAR_PLACES:], 1.0, 0.0, MULT, ADD)
        w1_codes = keep.tile([P, H], U32, name="w1_codes", tag="w1_codes_then_centres", align_bytes=64)
        w1_plane = after_middle.tile([P, H], U8, name="w1_plane", offset=0, align_bytes=64)
        nc.vector.quantize_mx(out=w1_codes[:].bitcast(FP8X4), scales=w1_plane[:], in_=w1_rounded[:].rearrange("p t m j -> p (t m j)"))

        xw_window = xw_all[:].bitcast(U32)
        xw_pick = keep.tile([P, S], U32, name="xw_pick", align_bytes=64)
        for first, last in zip(CUTS, CUTS[1:]):
            nc.vector.tensor_copy(xw_pick[:, first:last], xw_window.indirect(entries(offs_sb, first, last)))

        h = [keep.tile([P, S], F32, name="h%d" % t, align_bytes=64) for t in range(PACK)]

        def make_h(t, cuts, on_vector=False):
            first, last = cuts[0], cuts[-1]
            acc = next_bank(last - first)
            for a, b in zip(cuts, cuts[1:]):
                nc.tensor.matmul_mx(
                    out=acc[:, a - first : b - first], lhsT=w1_codes[:, t * P : (t + 1) * P].bitcast(FP8X4),
                    lhsT_scale=w1_plane[:, t * P : (t + 1) * P],
                    rhs=xw_pick[:, a:b].bitcast(FP8X4), rhs_scale=xs_pick[:, a:b], start=True, stop=True,
                )
            if on_vector:
                nc.vector.tensor_scalar_max(h[t][:, first:last], acc, 0.0)
            else:
                nc.scalar.activation(h[t][:, first:last], acc, RELU)

        def gather(dst, t, offsets, v0, v1, on_vector):
            window = h[t][:].indirect(entries(offsets, v0, v1))
            if on_vector:
                nc.vector.tensor_copy(dst, window)
            else:
                nc.scalar.activation(dst, window, COPY)

        def weave_views(dst, slabs):
            return dst.rearrange("p (c i) t -> p c t i", i=4), slabs.rearrange("p t (c i) -> p c t i", i=4)

        def weave_on_gpsimd(dst, slabs):
            nc.gpsimd.tensor_scalar(dst, slabs.rearrange("p t v -> p v t"), 1.0, 0.0, MULT, ADD)

        def quantize(woven, name, plane=None):
            count = woven.shape[1]
            codes = keep.tile([P, count], U32, name=name + "_codes", align_bytes=64)
            if plane is None:
                plane = keep.tile([P, count], U8, name=name + "_plane", align_bytes=64)
            nc.vector.quantize_mx(out=codes[:].bitcast(FP8X4), scales=plane[:], in_=woven.rearrange("p v t -> p (v t)"))
            return codes, plane

        for t in range(PACK):
            make_h(t, CUTS[0:2])
        for n in (1, 2):
            make_h(0, CUTS[n : n + 2])
            make_h(1, CUTS[n : n + 2])
        make_h(0, CUTS[3:5], on_vector=True)
        make_h(0, CUTS[4:6])
        make_h(1, CUTS[3:6])
        for t in (2, 3):
            make_h(t, (CUTS[1], CUTS[3]))
            make_h(t, CUTS[3:6])

        ends = keep.tile([P, 2, 2, PACK, HALF], BF16, name="ends", align_bytes=64)
        near0 = keep.tile([P, NEIGHBOURS, V], BF16, name="near0", tag="near0_then_centres", align_bytes=64)
        for d in range(NEIGHBOURS):
            gather(near0[:, d, :], 0, pos_sb[d], 0, V, True)
        low, high = [near0[:, d : d + 2, :].rearrange("p s (h v) -> p h s v", h=2) for d in (0, 2)]
        nc.vector.tensor_tensor(ends[:, :, :, 0, :], low, high, MAX)

        c_woven = keep.tile([P, V, PACK], BF16, name="c_woven", tag="near0_then_centres", align_bytes=64)
        c_slabs = keep.tile([P, PACK, V], BF16, name="c_slabs", tag="w1_codes_then_centres", align_bytes=64)
        for t in range(PACK):
            gather(c_slabs[:, t, :], t, cen_sb, 0, V, False)
        weave_on_gpsimd(c_woven[:], c_slabs[:])

        near = keep.tile([P, 2, PACK - 1, HALF], BF16, name="near_first", tag="near", align_bytes=64)
        for t in range(1, PACK):
            for d in range(NEIGHBOURS):
                dst = near[:, d, t - 1, :] if d < 2 else ends[:, 1, d - 2, t, :]
                if (t, d) == (3, 1):
                    gather(dst[:, :QUARTER], t, pos_sb[d], 0, QUARTER, True)
                    gather(dst[:, QUARTER:], t, pos_sb[d], QUARTER, HALF, False)
                else:
                    gather(dst, t, pos_sb[d], 0, HALF, t == 1 or d < 2)
        quarters = (slice(0, QUARTER), slice(QUARTER, HALF))
        for cols in quarters:
            nc.vector.tensor_tensor(ends[:, 0, :, 1:, cols], near[:, :, :, cols], ends[:, 1, :, 1:, cols], MAX)
        z_quarters = [
            shared.tile([P, PACK, QUARTER], BF16, name="z_quarter0", offset=0, align_bytes=64),
            keep.tile([P, PACK, QUARTER], BF16, name="z_quarter1", align_bytes=64),
        ]
        for cols, z_quarter in zip(quarters, z_quarters):
            nc.vector.tensor_tensor(z_quarter[:], ends[:, 0, 0, :, cols], ends[:, 0, 1, :, cols], MAX)
        z_woven = keep.tile([P, V, PACK], BF16, name="z_woven", align_bytes=64)
        for cols, z_quarter in zip(quarters, z_quarters):
            weave_on_gpsimd(z_woven[:, cols, :], z_quarter[:])

        first = keep.tile([P, PACK - 1, HALF], BF16, name="near_second", tag="near", align_bytes=64)
        middle = after_middle.tile([P, 2, PACK - 1, HALF], BF16, name="middle", offset=0, align_bytes=64)
        three, fourth = ends[:, 1, 0], ends[:, 1, 1]
        for t in range(1, PACK):
            gather(first[:, t - 1, :], t, pos_sb[0], HALF, V, True)
        for d in (1, 2):
            for t in range(1, PACK):
                gather(middle[:, d - 1, t - 1, :], t, pos_sb[d], HALF, V, False)
        for cols in quarters:
            for t in range(1, PACK):
                gather(fourth[:, t, cols], t, pos_sb[3], HALF + cols.start, HALF + cols.stop, False)
        two = shared.tile([P, PACK - 1, HALF], BF16, name="two", offset=HALF, align_bytes=64)
        z_third = keep.tile([P, PACK, QUARTER], BF16, name="z_third", tag="z_third_then_last_plane", align_bytes=64)
        z_fourth = keep.tile([P, PACK, QUARTER], BF16, name="z_fourth", align_bytes=64)
        nc.vector.tensor_tensor(two[:], first[:], middle[:, 0], MAX)
        planes = [shared.tile([P, HALF], U8, name="z0_plane", offset=0, align_bytes=64)]
        planes += [after_middle.tile([P, HALF], U8, name="c_plane%d" % n, offset=n * HALF, align_bytes=64) for n in range(2)]
        c_codes = [quantize(c_woven[:, :HALF, :], "c0", planes[0])]
        for cols in quarters:
            nc.vector.tensor_tensor(three[:, 1:, cols], two[:, :, cols], middle[:, 1, :, cols], MAX)
        nc.vector.tensor_tensor(z_third[:], three[:, :, :QUARTER], fourth[:, :, :QUARTER], MAX)
        nc.vector.tensor_tensor(z_fourth[:, 0:3, :], three[:, 0:3, QUARTER:], fourth[:, 0:3, QUARTER:], MAX)
        z_codes = [quantize(z_woven[:, :HALF, :], "z0", planes[1])]
        nc.vector.tensor_tensor(z_fourth[:, 3, :], three[:, 3, QUARTER:], fourth[:, 3, QUARTER:], MAX)
        nc.scalar.copy(*weave_views(z_woven[:, HALF : HALF + QUARTER, :], z_third[:]))
        c_codes.append(quantize(c_woven[:, HALF:, :], "c1", planes[2]))
        nc.vector.tensor_copy(*weave_views(z_woven[:, HALF + QUARTER :, :], z_fourth[:]))
        z_codes.append(quantize(z_woven[:, HALF : HALF + QUARTER, :], "z1"))
        last_plane = keep.tile([P, QUARTER], U8, name="last_plane", tag="z_third_then_last_plane", align_bytes=64)
        z_codes.append(quantize(z_woven[:, HALF + QUARTER :, :], "z2", last_plane))

        chunks = ((0, HALF), (HALF, HALF + QUARTER), (HALF + QUARTER, V))
        for (v0, v1), (codes, plane) in zip(chunks, z_codes):
            acc = next_bank(v1 - v0)
            centre_codes, centre_plane = c_codes[v0 // HALF]
            cols = slice(v0 % HALF, v0 % HALF + v1 - v0)
            nc.tensor.matmul_mx(
                out=acc, lhsT=w2_codes[:].bitcast(FP8X4), lhsT_scale=w2_plane[:],
                rhs=centre_codes[:, cols].bitcast(FP8X4), rhs_scale=centre_plane[:, cols], start=True, stop=False,
            )
            nc.tensor.matmul_mx(
                out=acc, lhsT=w3_codes[:].bitcast(FP8X4), lhsT_scale=w3_plane[:],
                rhs=codes[:].bitcast(FP8X4), rhs_scale=plane[:], start=False, stop=True,
            )
            result = keep.tile([P, v1 - v0], F32, name="result%d" % v0)
            if v1 == V:
                nc.vector.tensor_scalar_max(result[:], acc, 0.0)
            else:
                nc.scalar.activation(result[:], acc, RELU)
            nc.sync.dma_start(out=out[:, v0:v1], in_=result[:])
